import numpy as np
import ml_dtypes


def mxq(x, axis, fmt="e4m3"):
    dtype, down = {"e4m3": (ml_dtypes.float8_e4m3fn, 7), "e5m2": (ml_dtypes.float8_e5m2, 14)}[fmt]
    v = np.moveaxis(np.asarray(x, np.float32).astype(ml_dtypes.bfloat16).astype(np.float64), axis, -1)
    blocks = v.reshape(v.shape[:-1] + (-1, 32))
    amax = np.abs(blocks).max(-1, keepdims=True)
    byte = np.maximum(np.where(amax > 0, np.frexp(amax)[1] - 1 + 127, 0) - down, 1)
    scale = np.exp2(byte - 127.0)
    codes = (blocks / scale).astype(np.float32).astype(dtype).astype(np.float64)
    return np.moveaxis((codes * scale).reshape(v.shape), -1, axis)


WIDE = False


def mx_kscale(k):
    if not WIDE:
        return np.ones(k)
    levels = np.array([10, -10, 5, -5, 0])
    if k % 512:
        return np.exp2(np.random.permutation(np.resize(levels, k // 32))).repeat(32)
    a = np.empty((k // 512, 16))
    for p in range(k // 512):
        a[p, :8] = np.random.permutation(np.resize(levels, 8))
        for g in range(8):
            far = levels[np.abs(levels - a[p, g]) >= 10]
            a[p, g + 8] = far[np.random.randint(len(far))]
    return np.exp2(a.ravel()).repeat(32)


BF16 = ml_dtypes.bfloat16


def bf(x):
    return np.asarray(x, np.float32).astype(BF16)


def f64(x):
    return np.asarray(x).astype(np.float64)


E2M1 = np.array([0.0, 0.5, 1.0, 1.5, 2.0, 3.0, 4.0, 6.0, -0.0, -0.5, -1.0, -1.5, -2.0, -3.0, -4.0, -6.0])


def pack_weight(w, fmt):
    k, n = w.shape
    w = f64(bf(w)).reshape(k // 32, 32, n)
    amax = np.abs(w).max(1)
    if fmt == "e4m3":
        byte = np.frexp(amax)[1] - 1 + 127 - 7
    else:
        mant, ex = np.frexp(amax / 6.0)
        byte = np.where(mant > 0.5, ex, ex - 1) + 127
    byte = np.clip(np.where(amax > 0, byte, 1), 1, 254)
    scaled = (w * np.exp2(127.0 - byte)[:, None, :]).reshape(k, n).astype(np.float32)
    by_word = np.ascontiguousarray(scaled.reshape(k // 512, 128, 4, n).transpose(0, 1, 3, 2))
    if fmt == "e4m3":
        words = by_word.astype(ml_dtypes.float8_e4m3fn).view(np.uint8)
    else:
        c = by_word.astype(ml_dtypes.float4_e2m1fn).view(np.uint8) & 0xF
        words = c[..., 0::2] | (c[..., 1::2] << 4)
    return np.ascontiguousarray(words), np.ascontiguousarray(byte.astype(np.uint8).reshape(k // 512, 16, n))


def unpack_weight(words, scales, fmt):
    g, p, n, _ = words.shape
    if fmt == "e4m3":
        vals = np.ascontiguousarray(words).view(ml_dtypes.float8_e4m3fn).astype(np.float64)
    else:
        nib = np.empty((g, p, n, 4), np.uint8)
        nib[..., 0::2] = words & 0xF
        nib[..., 1::2] = words >> 4
        vals = E2M1[nib]
    vals = vals * np.repeat(np.exp2(scales.astype(np.float64) - 127.0), 8, axis=1)[..., None]
    return vals.transpose(0, 1, 3, 2).reshape(g * 512, n)
def pack4(w):
    words, scales = pack_weight(w, "e2m1")
    return words.reshape(words.shape[0], 128, -1), scales


def unpack4(words, scales):
    return unpack_weight(words.reshape(words.shape[0], 128, -1, 2), scales, "e2m1")


B, D, T, P, Q = 8, 512, 512, 512, 512


def scaled_softmax(e):
    p = np.exp(e - e.max(axis=-1, keepdims=True))
    return e.shape[-1] * (p / p.sum(axis=-1, keepdims=True))


def draw0():
    s, t = mx_kscale(D), mx_kscale(T)
    x = bf(np.random.standard_normal((B, D, T)) * s[None, :, None])
    w1_words, w1_scales = pack4((np.random.standard_normal((P, D)) / np.sqrt(D) / s[None, :]).T)
    g = bf((1.0 + 0.1 * np.random.standard_normal(T)) * t)
    w_words, w_scales = pack4(np.random.standard_normal((T, Q)) / np.sqrt(T) / t[:, None])
    w2_words, w2_scales = pack4(np.random.standard_normal((T, Q)) / np.sqrt(T) / t[:, None])
    return {
        "x": x,
        "w1_words": w1_words,
        "w1_scales": w1_scales,
        "g": g,
        "w_words": w_words,
        "w_scales": w_scales,
        "w2_words": w2_words,
        "w2_scales": w2_scales,
        "lam": bf(np.random.uniform(0.3, 0.7, P)),
        "bias": bf(0.4 * np.random.standard_normal((P, Q))),
    }


def core(x, w1_words, w1_scales, g, w_words, w_scales, w2_words, w2_scales, lam, bias):
    h0 = unpack4(w1_words, w1_scales).T @ mxq(f64(x), 1, "e4m3")
    h = h0 * f64(g)[None, None, :]
    hq = mxq(h, 2, "e4m3")
    u = hq @ unpack4(w2_words, w2_scales)
    e = hq @ unpack4(w_words, w_scales)
    a = scaled_softmax(e)
    mix = f64(lam)[None, :, None]
    z = mix * u * a + (1.0 - mix) * u + f64(bias)[None, :, :]
    return np.tanh(z)


def e4m3fn_bytes(y):
    return np.clip(np.asarray(y, np.float64), -448.0, 448.0).astype(np.float32).astype(ml_dtypes.float8_e4m3fn).view(np.uint8)


def e4m3fn_values(b):
    return np.asarray(b, np.uint8).view(ml_dtypes.float8_e4m3fn).astype(np.float64)


def setup_inputs():
    d = draw0()
    x0 = np.asarray(d['x']).astype(np.float64)
    s = (np.max(np.abs(x0), axis=(0, 2), keepdims=True) / 448.0).astype(np.float32)
    out = {}
    for k, v in d.items():
        if k == 'x':
            out['x_bytes'] = e4m3fn_bytes(x0 / s.astype(np.float64))
            out['x_scale'] = s
        else:
            out[k] = v
    return out


def reference(x_bytes, x_scale, w1_words, w1_scales, g, w_words, w_scales, w2_words, w2_scales, lam, bias):
    return core(e4m3fn_values(x_bytes) * x_scale.astype(np.float64), w1_words, w1_scales, g, w_words, w_scales, w2_words, w2_scales, lam, bias)

@@ -1,0 +1,342 @@
+from contextlib import ExitStack
+
+import concourse.mybir as mybir
+from concourse.masks import make_identity
+
+B, D, T, P, Q = 8, 512, 512, 512, 512
+FLOPS = 3 * 2 * B * D * T * P
+
+F32 = mybir.dt.float32
+BF16 = mybir.dt.bfloat16
+U32 = mybir.dt.uint32
+I32 = mybir.dt.int32
+U8 = mybir.dt.uint8
+FP8 = mybir.dt.float8_e4m3fn
+FP8X4 = mybir.dt.float8_e4m3fn_x4
+FP4X4 = mybir.dt.float4_e2m1fn_x4
+ALU = mybir.AluOpType
+ACT = mybir.ActivationFunctionType
+AX = mybir.AxisListType
+
+NP = 128
+NB = 4
+NT = B * NB
+TINY = 1e-15
+
+
+CHUNK_ENGINES = "ssgg"
+FIRST_CHUNK_ENGINES = "vvsg"
+
+
+def kind(i):
+    if i >= NT - 2:
+        return "v"
+    return "pe" if i % 2 == 0 else "g"
+
+
+def tile_temporalaugmentedbilinear_w4_kernel(
+    tc, x_bytes, x_scale, w1_words, w1_scales, g, w_words, w_scales, w2_words, w2_scales, lam, bias, out
+):
+    nc = tc.nc
+
+    with ExitStack() as ctx:
+        keep = ctx.enter_context(tc.tile_pool(name="keep", bufs=1))
+        work = ctx.enter_context(tc.tile_pool(name="work", bufs=2))
+        psum = ctx.enter_context(tc.psum_pool(name="psum", bufs=1))
+        ctx.enter_context(tc.manual_schedule())
+
+        warm = keep.tile([NP, 1], F32, name="warm")
+        nc.vector.memset(warm[:], 0.0)
+        warm_out = keep.tile([NP, 1], F32, name="warm_out")
+        nc.scalar.activation(out=warm_out[:], in_=warm[:], func=ACT.Exp)
+
+        planes = keep.tile([NP, 3, P], U8, name="planes", align_bytes=64)
+        nc.vector.memset(planes[:].rearrange("p a n -> p (a n)").bitcast(I32), 0)
+        lam_rows = keep.tile([NP, NP], BF16, name="lam_rows")
+        nc.vector.memset(lam_rows[:], 0.0)
+
+        ident_b = keep.tile([NP, NP], BF16, name="ident_b")
+        make_identity(nc, ident_b[:])
+        ident_f = keep.tile([NP, NP], F32, name="ident_f")
+        make_identity(nc, ident_f[:])
+
+        xb = []
+
+        def load_x(b):
+            codes_in = keep.tile([NP, 4, T], U8, name="codes_in%d" % b, align_bytes=64)
+            nc.sync.dma_start(out=codes_in[:], in_=x_bytes[b].rearrange("(p s) t -> p s t", s=4))
+            xb.append(codes_in)
+
+        words = []
+
+        def load_words(src, name):
+            wt = keep.tile([NP, 2 * P], U8, name=name, align_bytes=64)
+            nc.sync.dma_start(out=wt[:].bitcast(I32), in_=src[0].bitcast(I32))
+            words.append(wt)
+
+        def load_plane(idx, src):
+            for r in range(4):
+                nc.sync.dma_start(
+                    out=planes[r:NP:32, idx, :].bitcast(I32),
+                    in_=src[0, r:16:4, :].bitcast(I32),
+                )
+
+        load_x(0)
+        xs = keep.tile([NP, 4], F32, name="xs")
+        nc.sync.dma_start(out=xs[:], in_=x_scale.rearrange("o (p s) u -> p (o s u)", s=4))
+        load_words(w1_words, "w1_t")
+        load_plane(0, w1_scales)
+        gain = keep.tile([NP, 4], BF16, name="gain")
+        nc.sync.dma_start(out=gain[:], in_=g.rearrange("(p j) -> p j", j=4))
+        load_words(w_words, "w_t")
+        load_words(w2_words, "w2_t")
+        load_plane(1, w_scales)
+        load_plane(2, w2_scales)
+        load_x(1)
+        nc.sync.dma_start(out=lam_rows[0:NB, :], in_=lam.rearrange("(c p) -> c p", p=NP))
+        bias_t = keep.tile([NP, NB, Q], BF16, name="bias_t")
+        nc.sync.dma_start(out=bias_t[:], in_=bias.rearrange("(c p) q -> p c q", p=NP))
+        for b in range(2, B):
+            load_x(b)
+        w1_t, w_t, w2_t = words
+
+        lam_c = keep.tile([NP, NB], F32, name="lam_c")
+        cst = keep.tile([NP, NB, 2], F32, name="cst")
+
+        def row_constants():
+            lam_ps = psum.tile([NP, NP], BF16, name="lam_ps", tag="z", bufs=1)
+            nc.tensor.transpose(lam_ps[:], lam_rows[:], ident_b[:])
+            nc.vector.tensor_copy(out=lam_c[:], in_=lam_ps[:, 0:NB])
+            sq = keep.tile([NP, NB], F32, name="sq")
+            nc.vector.tensor_tensor(out=sq[:], in0=lam_c[:], in1=lam_c[:], op=ALU.mult)
+            nc.vector.tensor_scalar(
+                out=sq[:], in0=sq[:], scalar1=TINY * TINY, scalar2=2 * TINY, op0=ALU.is_lt, op1=ALU.mult
+            )
+            nc.vector.tensor_tensor(out=sq[:], in0=sq[:], in1=lam_c[:], op=ALU.add)
+            nc.vector.tensor_scalar(out=sq[:], in0=sq[:], scalar1=float(Q), scalar2=None, op0=ALU.mult)
+            nc.vector.reciprocal(out=cst[:, :, 1], in_=sq[:])
+            nc.vector.tensor_scalar(
+                out=lam_c[:], in0=lam_c[:], scalar1=-1.0, scalar2=1.0, op0=ALU.mult, op1=ALU.add
+            )
+            nc.vector.tensor_tensor(out=cst[:, :, 0], in0=lam_c[:], in1=cst[:, :, 1], op=ALU.mult)
+
+        xw, xg, xq, xqs = {}, {}, {}, {}
+
+        def widen(b, s):
+            if s == 0:
+                wide = work.tile([NP, 4, T], BF16, name="wide", bufs=2, align_bytes=64)
+                xw[b] = wide
+            src = xb[b][:, s, :].bitcast(FP8)
+            if b == 0 and s < 3:
+                nc.vector.tensor_scalar(
+                    out=xw[b][:, s, :], in0=src, scalar1=xs[:, s : s + 1], scalar2=None, op0=ALU.mult
+                )
+            else:
+                nc.scalar.activation(out=xw[b][:, s, :], in_=src, func=ACT.Copy, scale=xs[:, s : s + 1])
+
+        def interleave(b, c):
+            if c == 0:
+                grouped_x = work.tile([NP, 4, NP, 4], BF16, name="grouped_x", bufs=2, align_bytes=64)
+                xg[b] = grouped_x
+            o = xg[b][:, :, 32 * c : 32 * c + 32, :].rearrange("p j m s -> p m j s")
+            i = xw[b][:, :, NP * c : NP * c + NP].rearrange("p s (m j) -> p m j s", j=4)
+            eng = FIRST_CHUNK_ENGINES[c] if b == 0 else CHUNK_ENGINES[c]
+            if eng == "v":
+                nc.vector.tensor_copy(out=o, in_=i)
+            elif eng == "s":
+                nc.scalar.copy(out=o, in_=i)
+            else:
+                nc.gpsimd.tensor_scalar(out=o, in0=i, scalar1=1.0, scalar2=0.0, op0=ALU.mult, op1=ALU.add)
+
+        def quantise_x(b):
+            x_codes = work.tile([NP, T], U32, name="x_codes", bufs=2, align_bytes=64)
+            x_plane = work.tile([NP, T], U8, name="x_plane", bufs=2, align_bytes=64)
+            nc.vector.quantize_mx(
+                out=x_codes[:].bitcast(FP8X4),
+                scales=x_plane[:],
+                in_=xg[b][:].rearrange("p j m s -> p (j m s)"),
+            )
+            xq[b], xqs[b] = x_codes, x_plane
+
+        hp, hg, hq, hqs = {}, {}, {}, {}
+
+        def first_mm(i):
+            b, pb = divmod(i, NB)
+            h_ps = psum.tile([NP, 4, NP], F32, name="h_ps", bufs=2)
+            hp[i] = h_ps
+            for j in range(4):
+                nc.tensor.matmul_mx(
+                    out=h_ps[:, j, :],
+                    lhsT=xq[b][:, NP * j : NP * j + NP].bitcast(FP8X4),
+                    lhsT_scale=xqs[b][:, NP * j : NP * j + NP],
+                    rhs=w1_t[:, 2 * NP * pb : 2 * NP * (pb + 1)].bitcast(FP4X4),
+                    rhs_scale=planes[:, 0, NP * pb : NP * (pb + 1)],
+                    start=True,
+                    stop=True,
+                )
+
+        def apply_gain(i):
+            grouped_h = work.tile([NP, NP, 4], BF16, name="grouped_h", bufs=3, align_bytes=64)
+            hg[i] = grouped_h
+            nc.vector.tensor_tensor(
+                out=grouped_h[:],
+                in0=hp[i][:].rearrange("p j n -> p n j"),
+                in1=gain[:].unsqueeze(1).to_broadcast([NP, NP, 4]),
+                op=ALU.mult,
+            )
+
+        def quantise_h(i):
+            h_codes = work.tile([NP, NP], U32, name="h_codes", bufs=3, align_bytes=64)
+            h_plane = work.tile([NP, NP], U8, name="h_plane", bufs=3, align_bytes=64)
+            nc.vector.quantize_mx(
+                out=h_codes[:].bitcast(FP8X4), scales=h_plane[:], in_=hg[i][:].rearrange("p n j -> p (n j)")
+            )
+            hq[i], hqs[i] = h_codes, h_plane
+
+        ep, up = {}, {}
+
+        def second_mm(i, which):
+            if which == 1:
+                e_ps = psum.tile([NP, Q], F32, name="e_ps", bufs=2)
+                ep[i] = e_ps
+                dst, wt = e_ps, w_t
+            else:
+                u_ps = psum.tile([NP, Q], F32, name="u_ps", bufs=3)
+                up[i] = u_ps
+                dst, wt = u_ps, w2_t
+            nc.tensor.matmul_mx(
+                out=dst[:],
+                lhsT=hq[i][:].bitcast(FP8X4),
+                lhsT_scale=hqs[i][:],
+                rhs=wt[:].bitcast(FP4X4),
+                rhs_scale=planes[:, which, :],
+                start=True,
+                stop=True,
+            )
+
+        nmax, ex, sm, dr, cf, vv, zz, ot = {}, {}, {}, {}, {}, {}, {}, {}
+
+        def row_max(i):
+            neg_max = work.tile([NP, 1], F32, name="neg_max", bufs=4)
+            nmax[i] = neg_max
+            nc.vector.tensor_reduce(out=neg_max[:], in_=ep[i][:], axis=AX.X, op=ALU.max, negate=True)
+
+        def exponent(i):
+            e_sb = work.tile([NP, Q], F32, name="e_sb", bufs=3)
+            e_sum = work.tile([NP, 1], F32, name="e_sum", bufs=6)
+            ex[i], sm[i] = e_sb, e_sum
+            nc.scalar.activation(
+                out=e_sb[:], in_=ep[i][:], func=ACT.Exp, bias=nmax[i][:], scale=1.0, accum_out=e_sum[:]
+            )
+
+        def row_factors(i):
+            if i % 2 == 1 or i == 0:
+                d_rc = work.tile([NP, 2, 2], F32, name="d_rc", bufs=4)
+                dr[i] = dr[i + i % 2] = d_rc
+            nc.scalar.activation(out=dr[i][:, i % 2, :], in_=cst[:, i % NB, :], func=ACT.Copy, scale=sm[i][:])
+
+        def product(i):
+            v_sb = work.tile([NP, Q], F32, name="v_sb", bufs=4)
+            vv[i] = v_sb
+            nc.vector.scalar_tensor_tensor(
+                out=v_sb[:], in0=ex[i][:], scalar=dr[i][:, i % 2, 0:1], in1=up[i][:], op0=ALU.add, op1=ALU.mult
+            )
+
+        def row_coeff(i):
+            if i % 2 == 1 and i < NT - 1:
+                return
+            coeff = work.tile([NP, 2], F32, name="coeff", bufs=4)
+            if i % 2 == 1 or i == 0:
+                cf[i] = coeff[:, i % 2 : i % 2 + 1]
+                nc.vector.reciprocal(out=cf[i], in_=dr[i][:, i % 2, 1:2])
+            else:
+                cf[i - 1], cf[i] = coeff[:, 1:2], coeff[:, 0:1]
+                nc.vector.reciprocal(out=coeff[:], in_=dr[i][:, :, 1])
+
+        dg = {}
+
+        def gps(i):
+            pb = i % NB
+            if kind(i) == "v":
+                z_v = work.tile([NP, Q], F32, name="z_v", bufs=2)
+                zz[i] = z_v
+                nc.vector.scalar_tensor_tensor(
+                    out=z_v[:], in0=vv[i][:], scalar=cf[i], in1=bias_t[:, pb, :], op0=ALU.mult, op1=ALU.add
+                )
+            elif kind(i) == "pe":
+                diag = work.tile([NP, NP], F32, name="diag", bufs=3)
+                dg[i] = diag
+                nc.gpsimd.tensor_scalar(
+                    out=diag[:], in0=ident_f[:], scalar1=cf[i], scalar2=0.0, op0=ALU.mult, op1=ALU.add
+                )
+            else:
+                b_sc = work.tile([NP, Q], F32, name="b_sc", bufs=2)
+                nc.gpsimd.tensor_scalar(
+                    out=b_sc[:],
+                    in0=bias_t[:, pb, :],
+                    scalar1=sm[i][:],
+                    scalar2=cst[:, pb, 1:2],
+                    op0=ALU.mult,
+                    op1=ALU.mult,
+                )
+                z_sb = work.tile([NP, Q], F32, name="z_sb", bufs=2)
+                zz[i] = z_sb
+                nc.gpsimd.tensor_tensor(out=z_sb[:], in0=vv[i][:], in1=b_sc[:], op=ALU.add)
+
+        def bias_mm(i):
+            z_ps = psum.tile([NP, Q], F32, name="z_ps", tag="z", bufs=1)
+            zz[i] = z_ps
+            nc.tensor.matmul(z_ps[:], lhsT=ident_b[:], rhs=bias_t[:, i % NB, :], start=True, stop=False)
+            nc.tensor.matmul(z_ps[:], lhsT=dg[i][:], rhs=vv[i][:], start=False, stop=True)
+
+        def finish(i):
+            b, pb = divmod(i, NB)
+            o_sb = work.tile([NP, Q], F32, name="o_sb", bufs=4)
+            scale = cf[i] if kind(i) == "g" else 1.0
+            nc.scalar.activation(out=o_sb[:], in_=zz[i][:], func=ACT.Tanh, scale=scale)
+            nc.sync.dma_start(out=out[b, NP * pb : NP * (pb + 1), :], in_=o_sb[:])
+
+        def valid(i):
+            return 0 <= i < NT
+
+        for s in range(4):
+            widen(0, s)
+        for c in range(4):
+            interleave(0, c)
+        quantise_x(0)
+        for n in range(-7, NT + 4):
+            if valid(n):
+                row_max(n)
+            if valid(n - 3):
+                finish(n - 3)
+            if valid(n):
+                exponent(n)
+            if valid(n + 1):
+                quantise_h(n + 1)
+                second_mm(n + 1, 1)
+            b, s = divmod(n + 11, 4)
+            if 1 <= b < B:
+                widen(b, s)
+            if valid(n):
+                row_factors(n)
+            if valid(n - 1):
+                product(n - 1)
+                row_coeff(n - 1)
+            if valid(n + 1):
+                second_mm(n + 1, 2)
+            if valid(n + 2):
+                apply_gain(n + 2)
+            b, c = divmod(n + 7, 4)
+            if 1 <= b < B:
+                interleave(b, c)
+            b, c = divmod(n + 3, 4)
+            if 1 <= b < B and c == 0:
+                quantise_x(b)
+            if valid(n + 3):
+                first_mm(n + 3)
+            if n == -2:
+                row_constants()
+            if valid(n - 1):
+                gps(n - 1)
+            if valid(n - 2) and kind(n - 2) == "pe":
+                bias_mm(n - 2)

@@ -24,8 +24,8 @@ NT = B * NB
 TINY = 1e-15
 
 
-CHUNK_ENGINES = "ssgg"
-FIRST_CHUNK_ENGINES = "vvsg"
+CHUNK_ENGINES = ("vvsg", "vvgg", "sgsg")
+WIDEN_ENGINES = ("vvvs", "vvvv", "ssss")
 
 
 def kind(i):
@@ -84,16 +84,16 @@ def tile_temporalaugmentedbilinear_w4_kernel(
         load_x(0)
         xs = keep.tile([NP, 4], F32, name="xs")
         nc.sync.dma_start(out=xs[:], in_=x_scale.rearrange("o (p s) u -> p (o s u)", s=4))
+        nc.sync.dma_start(out=lam_rows[0:NB, :], in_=lam.rearrange("(c p) -> c p", p=NP))
         load_words(w1_words, "w1_t")
         load_plane(0, w1_scales)
         gain = keep.tile([NP, 4], BF16, name="gain")
         nc.sync.dma_start(out=gain[:], in_=g.rearrange("(p j) -> p j", j=4))
         load_words(w_words, "w_t")
-        load_words(w2_words, "w2_t")
         load_plane(1, w_scales)
+        load_words(w2_words, "w2_t")
         load_plane(2, w2_scales)
         load_x(1)
-        nc.sync.dma_start(out=lam_rows[0:NB, :], in_=lam.rearrange("(c p) -> c p", p=NP))
         bias_t = keep.tile([NP, NB, Q], BF16, name="bias_t")
         nc.sync.dma_start(out=bias_t[:], in_=bias.rearrange("(c p) q -> p c q", p=NP))
         for b in range(2, B):
@@ -103,22 +103,25 @@ def tile_temporalaugmentedbilinear_w4_kernel(
         lam_c = keep.tile([NP, NB], F32, name="lam_c")
         cst = keep.tile([NP, NB, 2], F32, name="cst")
 
-        def row_constants():
-            lam_ps = psum.tile([NP, NP], BF16, name="lam_ps", tag="z", bufs=1)
-            nc.tensor.transpose(lam_ps[:], lam_rows[:], ident_b[:])
-            nc.vector.tensor_copy(out=lam_c[:], in_=lam_ps[:, 0:NB])
-            sq = keep.tile([NP, NB], F32, name="sq")
-            nc.vector.tensor_tensor(out=sq[:], in0=lam_c[:], in1=lam_c[:], op=ALU.mult)
-            nc.vector.tensor_scalar(
-                out=sq[:], in0=sq[:], scalar1=TINY * TINY, scalar2=2 * TINY, op0=ALU.is_lt, op1=ALU.mult
+        rowk = keep.tile([NP, NB], F32, name="rowk")
+        lam_ps = psum.tile([NP, NP], BF16, name="lam_ps", tag="z", bufs=1)
+
+        def row_constants_1():
+            nc.gpsimd.tensor_tensor(out=rowk[:], in0=lam_c[:], in1=lam_c[:], op=ALU.mult)
+            nc.gpsimd.tensor_scalar(
+                out=rowk[:], in0=rowk[:], scalar1=TINY * TINY, scalar2=2 * TINY, op0=ALU.is_lt, op1=ALU.mult
             )
-            nc.vector.tensor_tensor(out=sq[:], in0=sq[:], in1=lam_c[:], op=ALU.add)
-            nc.vector.tensor_scalar(out=sq[:], in0=sq[:], scalar1=float(Q), scalar2=None, op0=ALU.mult)
-            nc.vector.reciprocal(out=cst[:, :, 1], in_=sq[:])
-            nc.vector.tensor_scalar(
+            nc.gpsimd.tensor_tensor(out=rowk[:], in0=rowk[:], in1=lam_c[:], op=ALU.add)
+            nc.gpsimd.tensor_scalar(
+                out=rowk[:], in0=rowk[:], scalar1=float(Q), scalar2=0.0, op0=ALU.mult, op1=ALU.add
+            )
+            nc.gpsimd.tensor_scalar(
                 out=lam_c[:], in0=lam_c[:], scalar1=-1.0, scalar2=1.0, op0=ALU.mult, op1=ALU.add
             )
-            nc.vector.tensor_tensor(out=cst[:, :, 0], in0=lam_c[:], in1=cst[:, :, 1], op=ALU.mult)
+
+        def row_constants_2():
+            nc.vector.reciprocal(out=cst[:, :, 1], in_=rowk[:])
+            nc.gpsimd.tensor_tensor(out=cst[:, :, 0], in0=lam_c[:], in1=cst[:, :, 1], op=ALU.mult)
 
         xw, xg, xq, xqs = {}, {}, {}, {}
 
@@ -127,7 +130,7 @@ def tile_temporalaugmentedbilinear_w4_kernel(
                 wide = work.tile([NP, 4, T], BF16, name="wide", bufs=2, align_bytes=64)
                 xw[b] = wide
             src = xb[b][:, s, :].bitcast(FP8)
-            if b == 0 and s < 3:
+            if WIDEN_ENGINES[min(b, 2)][s] == "v":
                 nc.vector.tensor_scalar(
                     out=xw[b][:, s, :], in0=src, scalar1=xs[:, s : s + 1], scalar2=None, op0=ALU.mult
                 )
@@ -140,7 +143,7 @@ def tile_temporalaugmentedbilinear_w4_kernel(
                 xg[b] = grouped_x
             o = xg[b][:, :, 32 * c : 32 * c + 32, :].rearrange("p j m s -> p m j s")
             i = xw[b][:, :, NP * c : NP * c + NP].rearrange("p s (m j) -> p m j s", j=4)
-            eng = FIRST_CHUNK_ENGINES[c] if b == 0 else CHUNK_ENGINES[c]
+            eng = CHUNK_ENGINES[min(b, 2)][c]
             if eng == "v":
                 nc.vector.tensor_copy(out=o, in_=i)
             elif eng == "s":
@@ -176,20 +179,23 @@ def tile_temporalaugmentedbilinear_w4_kernel(
                 )
 
         def apply_gain(i):
-            grouped_h = work.tile([NP, NP, 4], BF16, name="grouped_h", bufs=3, align_bytes=64)
-            hg[i] = grouped_h
+            if i % 2 == 0:
+                grouped_h = work.tile([NP, 2, NP, 4], BF16, name="grouped_h", bufs=2, align_bytes=64)
+                hg[i // 2] = grouped_h
             nc.vector.tensor_tensor(
-                out=grouped_h[:],
+                out=hg[i // 2][:, i % 2, :, :],
                 in0=hp[i][:].rearrange("p j n -> p n j"),
                 in1=gain[:].unsqueeze(1).to_broadcast([NP, NP, 4]),
                 op=ALU.mult,
             )
 
         def quantise_h(i):
-            h_codes = work.tile([NP, NP], U32, name="h_codes", bufs=3, align_bytes=64)
-            h_plane = work.tile([NP, NP], U8, name="h_plane", bufs=3, align_bytes=64)
+            h_codes = work.tile([NP, 2 * NP], U32, name="h_codes", bufs=3, align_bytes=64)
+            h_plane = work.tile([NP, 2 * NP], U8, name="h_plane", bufs=3, align_bytes=64)
             nc.vector.quantize_mx(
-                out=h_codes[:].bitcast(FP8X4), scales=h_plane[:], in_=hg[i][:].rearrange("p n j -> p (n j)")
+                out=h_codes[:].bitcast(FP8X4),
+                scales=h_plane[:],
+                in_=hg[i][:].rearrange("p u n j -> p (u n j)"),
             )
             hq[i], hqs[i] = h_codes, h_plane
 
@@ -197,17 +203,17 @@ def tile_temporalaugmentedbilinear_w4_kernel(
 
         def second_mm(i, which):
             if which == 1:
-                e_ps = psum.tile([NP, Q], F32, name="e_ps", bufs=2)
+                e_ps = psum.tile([NP, Q], F32, name="e_ps", bufs=3)
                 ep[i] = e_ps
                 dst, wt = e_ps, w_t
             else:
-                u_ps = psum.tile([NP, Q], F32, name="u_ps", bufs=3)
+                u_ps = psum.tile([NP, Q], F32, name="u_ps", bufs=2)
                 up[i] = u_ps
                 dst, wt = u_ps, w2_t
             nc.tensor.matmul_mx(
                 out=dst[:],
-                lhsT=hq[i][:].bitcast(FP8X4),
-                lhsT_scale=hqs[i][:],
+                lhsT=hq[i // 2][:, NP * (i % 2) : NP * (i % 2) + NP].bitcast(FP8X4),
+                lhsT_scale=hqs[i // 2][:, NP * (i % 2) : NP * (i % 2) + NP],
                 rhs=wt[:].bitcast(FP4X4),
                 rhs_scale=planes[:, which, :],
                 start=True,
@@ -222,66 +228,63 @@ def tile_temporalaugmentedbilinear_w4_kernel(
             nc.vector.tensor_reduce(out=neg_max[:], in_=ep[i][:], axis=AX.X, op=ALU.max, negate=True)
 
         def exponent(i):
-            e_sb = work.tile([NP, Q], F32, name="e_sb", bufs=3)
-            e_sum = work.tile([NP, 1], F32, name="e_sum", bufs=6)
+            e_sb = work.tile([NP, Q], F32, name="e_sb", bufs=4)
+            e_sum = work.tile([NP, 1], F32, name="e_sum", bufs=10)
             ex[i], sm[i] = e_sb, e_sum
             nc.scalar.activation(
                 out=e_sb[:], in_=ep[i][:], func=ACT.Exp, bias=nmax[i][:], scale=1.0, accum_out=e_sum[:]
             )
 
         def row_factors(i):
-            if i % 2 == 1 or i == 0:
-                d_rc = work.tile([NP, 2, 2], F32, name="d_rc", bufs=4)
-                dr[i] = dr[i + i % 2] = d_rc
+            if i % 2 == 0:
+                d_rc = work.tile([NP, 2, 2], F32, name="d_rc", bufs=6)
+                dr[i] = dr[i + 1] = d_rc
             nc.scalar.activation(out=dr[i][:, i % 2, :], in_=cst[:, i % NB, :], func=ACT.Copy, scale=sm[i][:])
 
         def product(i):
-            v_sb = work.tile([NP, Q], F32, name="v_sb", bufs=4)
+            v_sb = work.tile([NP, Q], F32, name="v_sb", bufs=8)
             vv[i] = v_sb
             nc.vector.scalar_tensor_tensor(
                 out=v_sb[:], in0=ex[i][:], scalar=dr[i][:, i % 2, 0:1], in1=up[i][:], op0=ALU.add, op1=ALU.mult
             )
 
         def row_coeff(i):
-            if i % 2 == 1 and i < NT - 1:
-                return
-            coeff = work.tile([NP, 2], F32, name="coeff", bufs=4)
-            if i % 2 == 1 or i == 0:
-                cf[i] = coeff[:, i % 2 : i % 2 + 1]
-                nc.vector.reciprocal(out=cf[i], in_=dr[i][:, i % 2, 1:2])
-            else:
-                cf[i - 1], cf[i] = coeff[:, 1:2], coeff[:, 0:1]
-                nc.vector.reciprocal(out=coeff[:], in_=dr[i][:, :, 1])
+            coeff = work.tile([NP, 2], F32, name="coeff", bufs=6)
+            cf[i], cf[i + 1] = coeff[:, 0:1], coeff[:, 1:2]
+            nc.vector.reciprocal(out=coeff[:], in_=dr[i][:, :, 1])
 
-        dg = {}
+        dg, bs = {}, {}
 
-        def gps(i):
-            pb = i % NB
-            if kind(i) == "v":
-                z_v = work.tile([NP, Q], F32, name="z_v", bufs=2)
-                zz[i] = z_v
-                nc.vector.scalar_tensor_tensor(
-                    out=z_v[:], in0=vv[i][:], scalar=cf[i], in1=bias_t[:, pb, :], op0=ALU.mult, op1=ALU.add
-                )
-            elif kind(i) == "pe":
-                diag = work.tile([NP, NP], F32, name="diag", bufs=3)
-                dg[i] = diag
-                nc.gpsimd.tensor_scalar(
-                    out=diag[:], in0=ident_f[:], scalar1=cf[i], scalar2=0.0, op0=ALU.mult, op1=ALU.add
-                )
-            else:
-                b_sc = work.tile([NP, Q], F32, name="b_sc", bufs=2)
-                nc.gpsimd.tensor_scalar(
-                    out=b_sc[:],
-                    in0=bias_t[:, pb, :],
-                    scalar1=sm[i][:],
-                    scalar2=cst[:, pb, 1:2],
-                    op0=ALU.mult,
-                    op1=ALU.mult,
-                )
-                z_sb = work.tile([NP, Q], F32, name="z_sb", bufs=2)
-                zz[i] = z_sb
-                nc.gpsimd.tensor_tensor(out=z_sb[:], in0=vv[i][:], in1=b_sc[:], op=ALU.add)
+        def scale_bias(i):
+            b_sc = work.tile([NP, Q], F32, name="b_sc", bufs=3)
+            bs[i] = b_sc
+            nc.gpsimd.tensor_scalar(
+                out=b_sc[:],
+                in0=bias_t[:, i % NB, :],
+                scalar1=dr[i][:, i % 2, 1:2],
+                scalar2=0.0,
+                op0=ALU.mult,
+                op1=ALU.add,
+            )
+
+        def add_bias(i):
+            z_sb = work.tile([NP, Q], F32, name="z_sb", bufs=3)
+            zz[i] = z_sb
+            nc.gpsimd.tensor_tensor(out=z_sb[:], in0=vv[i][:], in1=bs[i][:], op=ALU.add)
+
+        def make_diag(i):
+            diag = work.tile([NP, NP], F32, name="diag", bufs=3)
+            dg[i] = diag
+            nc.gpsimd.tensor_scalar(
+                out=diag[:], in0=ident_f[:], scalar1=cf[i], scalar2=0.0, op0=ALU.mult, op1=ALU.add
+            )
+
+        def add_bias_v(i):
+            z_v = work.tile([NP, Q], F32, name="z_v", bufs=2)
+            zz[i] = z_v
+            nc.vector.scalar_tensor_tensor(
+                out=z_v[:], in0=vv[i][:], scalar=cf[i], in1=bias_t[:, i % NB, :], op0=ALU.mult, op1=ALU.add
+            )
 
         def bias_mm(i):
             z_ps = psum.tile([NP, Q], F32, name="z_ps", tag="z", bufs=1)
@@ -299,44 +302,64 @@ def tile_temporalaugmentedbilinear_w4_kernel(
         def valid(i):
             return 0 <= i < NT
 
+        def is_kind(i, k):
+            return valid(i) and kind(i) == k
+
+        nc.tensor.transpose(lam_ps[:], lam_rows[:], ident_b[:])
         for s in range(4):
             widen(0, s)
+        nc.vector.tensor_copy(out=lam_c[:], in_=lam_ps[:, 0:NB])
         for c in range(4):
             interleave(0, c)
+        row_constants_1()
         quantise_x(0)
-        for n in range(-7, NT + 4):
+        row_constants_2()
+
+        for n in range(-4, NT + 7):
             if valid(n):
                 row_max(n)
-            if valid(n - 3):
-                finish(n - 3)
-            if valid(n):
-                exponent(n)
-            if valid(n + 1):
-                quantise_h(n + 1)
-                second_mm(n + 1, 1)
-            b, s = divmod(n + 11, 4)
-            if 1 <= b < B:
-                widen(b, s)
-            if valid(n):
-                row_factors(n)
-            if valid(n - 1):
-                product(n - 1)
-                row_coeff(n - 1)
-            if valid(n + 1):
-                second_mm(n + 1, 2)
-            if valid(n + 2):
-                apply_gain(n + 2)
-            b, c = divmod(n + 7, 4)
-            if 1 <= b < B:
-                interleave(b, c)
-            b, c = divmod(n + 3, 4)
+            b, c = divmod(n + 4, 4)
             if 1 <= b < B and c == 0:
                 quantise_x(b)
-            if valid(n + 3):
-                first_mm(n + 3)
-            if n == -2:
-                row_constants()
+            if valid(n + 4):
+                first_mm(n + 4)
+            if n % 2 == 0 and valid(n + 2):
+                quantise_h(n // 2 + 1)
+            if valid(n + 2):
+                second_mm(n + 2, 1)
+            if n % 2 == 0 and valid(n - 4):
+                row_coeff(n - 4)
             if valid(n - 1):
-                gps(n - 1)
-            if valid(n - 2) and kind(n - 2) == "pe":
-                bias_mm(n - 2)
+                second_mm(n - 1, 2)
+            if valid(n):
+                exponent(n)
+            if valid(n - 6):
+                finish(n - 6)
+            b, s = divmod(n + 12, 4)
+            if 2 <= b < B:
+                widen(b, s)
+            if valid(n - 0):
+                row_factors(n - 0)
+            if valid(n - 2):
+                product(n - 2)
+            if is_kind(n - 4, "pe"):
+                make_diag(n - 4)
+            if is_kind(n - 5, "g"):
+                scale_bias(n - 5)
+            if is_kind(n - 5, "g"):
+                add_bias(n - 5)
+            if is_kind(n - 4, "v"):
+                add_bias_v(n - 4)
+            if valid(n + 4):
+                apply_gain(n + 4)
+            if n == -3:
+                for s in range(4):
+                    widen(1, s)
+            if n == -1:
+                for c in range(4):
+                    interleave(1, c)
+            b, c = divmod(n + 8, 4)
+            if 2 <= b < B:
+                interleave(b, c)
+            if is_kind(n - 5, "pe"):
+                bias_mm(n - 5)

@@ -24,14 +24,17 @@ NT = B * NB
 TINY = 1e-15
 
 
-CHUNK_ENGINES = ("vvsg", "vvgg", "sgsg")
+CHUNK_ENGINES = ("vvsg", "vvgg", "sssg")
 WIDEN_ENGINES = ("vvvs", "vvvv", "ssss")
+
+
+KINDS = "gpgv"
 
 
 def kind(i):
     if i >= NT - 2:
         return "v"
-    return "pe" if i % 2 == 0 else "g"
+    return {"p": "pe", "g": "g", "v": "v"}[KINDS[i % len(KINDS)]]
 
 
 def tile_temporalaugmentedbilinear_w4_kernel(
@@ -127,7 +130,7 @@ def tile_temporalaugmentedbilinear_w4_kernel(
 
         def widen(b, s):
             if s == 0:
-                wide = work.tile([NP, 4, T], BF16, name="wide", bufs=2, align_bytes=64)
+                wide = work.tile([NP, 4, T], BF16, name="wide", bufs=3, align_bytes=64)
                 xw[b] = wide
             src = xb[b][:, s, :].bitcast(FP8)
             if WIDEN_ENGINES[min(b, 2)][s] == "v":
@@ -139,7 +142,7 @@ def tile_temporalaugmentedbilinear_w4_kernel(
 
         def interleave(b, c):
             if c == 0:
-                grouped_x = work.tile([NP, 4, NP, 4], BF16, name="grouped_x", bufs=2, align_bytes=64)
+                grouped_x = work.tile([NP, 4, NP, 4], BF16, name="grouped_x", bufs=3, align_bytes=64)
                 xg[b] = grouped_x
             o = xg[b][:, :, 32 * c : 32 * c + 32, :].rearrange("p j m s -> p m j s")
             i = xw[b][:, :, NP * c : NP * c + NP].rearrange("p s (m j) -> p m j s", j=4)
@@ -316,50 +319,50 @@ def tile_temporalaugmentedbilinear_w4_kernel(
         row_constants_2()
 
         for n in range(-4, NT + 7):
-            if valid(n):
-                row_max(n)
+            b, c = divmod(n + 8, 4)
+            if 2 <= b < B:
+                interleave(b, c)
             b, c = divmod(n + 4, 4)
             if 1 <= b < B and c == 0:
                 quantise_x(b)
-            if valid(n + 4):
-                first_mm(n + 4)
-            if n % 2 == 0 and valid(n + 2):
-                quantise_h(n // 2 + 1)
-            if valid(n + 2):
-                second_mm(n + 2, 1)
-            if n % 2 == 0 and valid(n - 4):
-                row_coeff(n - 4)
-            if valid(n - 1):
-                second_mm(n - 1, 2)
-            if valid(n):
-                exponent(n)
-            if valid(n - 6):
-                finish(n - 6)
+            if is_kind(n - 4, "g"):
+                add_bias(n - 4)
             b, s = divmod(n + 12, 4)
             if 2 <= b < B:
                 widen(b, s)
-            if valid(n - 0):
-                row_factors(n - 0)
-            if valid(n - 2):
-                product(n - 2)
-            if is_kind(n - 4, "pe"):
-                make_diag(n - 4)
-            if is_kind(n - 5, "g"):
-                scale_bias(n - 5)
-            if is_kind(n - 5, "g"):
-                add_bias(n - 5)
+            if valid(n + 4):
+                first_mm(n + 4)
+            if valid(n):
+                row_max(n)
+            if valid(n):
+                exponent(n)
             if is_kind(n - 4, "v"):
                 add_bias_v(n - 4)
-            if valid(n + 4):
-                apply_gain(n + 4)
-            if n == -3:
+            if valid(n - 6):
+                finish(n - 6)
+            if n == -4:
                 for s in range(4):
                     widen(1, s)
             if n == -1:
                 for c in range(4):
                     interleave(1, c)
-            b, c = divmod(n + 8, 4)
-            if 2 <= b < B:
-                interleave(b, c)
+            if valid(n - 2):
+                product(n - 2)
+            if is_kind(n - 2, "g"):
+                scale_bias(n - 2)
+            if is_kind(n - 3, "pe"):
+                make_diag(n - 3)
+            if n % 2 == 0 and valid(n + 2):
+                quantise_h(n // 2 + 1)
+            if n % 2 == 0 and valid(n - 2):
+                row_coeff(n - 2)
+            if valid(n + 4):
+                apply_gain(n + 4)
+            if valid(n):
+                row_factors(n)
             if is_kind(n - 5, "pe"):
                 bias_mm(n - 5)
+            if valid(n - 1):
+                second_mm(n - 1, 2)
+            if valid(n + 2):
+                second_mm(n + 2, 1)

@@ -24,17 +24,25 @@ NT = B * NB
 TINY = 1e-15
 
 
-CHUNK_ENGINES = ("vvsg", "vvgg", "sssg")
-WIDEN_ENGINES = ("vvvs", "vvvv", "ssss")
+CHUNK_ENGINES = ("vvvs", "ssss", "sssg")
+WIDEN_ENGINES = ("vvvs", "svvv", "ssss")
 
 
-KINDS = "gpgv"
+def column_parts(i):
+    return (slice(0, 256), slice(256, 512)) if i >= NT - 1 else (slice(0, 512),)
+
+
+KINDS = "gpgvgpgg"
+TAIL = 24
+TAIL_KINDS = "gvgvgvvv"
 
 
 def kind(i):
-    if i >= NT - 2:
-        return "v"
-    return {"p": "pe", "g": "g", "v": "v"}[KINDS[i % len(KINDS)]]
+    return {"p": "pe", "g": "g", "v": "v"}[TAIL_KINDS[i - TAIL] if i >= TAIL else KINDS[i % len(KINDS)]]
+
+
+def finish_step(i):
+    return i + 5 - min(2, max(0, (i - 21) // 2))
 
 
 def tile_temporalaugmentedbilinear_w4_kernel(
@@ -87,19 +95,20 @@ def tile_temporalaugmentedbilinear_w4_kernel(
         load_x(0)
         xs = keep.tile([NP, 4], F32, name="xs")
         nc.sync.dma_start(out=xs[:], in_=x_scale.rearrange("o (p s) u -> p (o s u)", s=4))
-        nc.sync.dma_start(out=lam_rows[0:NB, :], in_=lam.rearrange("(c p) -> c p", p=NP))
         load_words(w1_words, "w1_t")
         load_plane(0, w1_scales)
+        load_x(1)
         gain = keep.tile([NP, 4], BF16, name="gain")
         nc.sync.dma_start(out=gain[:], in_=g.rearrange("(p j) -> p j", j=4))
         load_words(w_words, "w_t")
         load_plane(1, w_scales)
+        nc.sync.dma_start(out=lam_rows[0:NB, :], in_=lam.rearrange("(c p) -> c p", p=NP))
         load_words(w2_words, "w2_t")
         load_plane(2, w2_scales)
-        load_x(1)
+        load_x(2)
         bias_t = keep.tile([NP, NB, Q], BF16, name="bias_t")
         nc.sync.dma_start(out=bias_t[:], in_=bias.rearrange("(c p) q -> p c q", p=NP))
-        for b in range(2, B):
+        for b in range(3, B):
             load_x(b)
         w1_t, w_t, w2_t = words
 
@@ -110,6 +119,8 @@ def tile_temporalaugmentedbilinear_w4_kernel(
         lam_ps = psum.tile([NP, NP], BF16, name="lam_ps", tag="z", bufs=1)
 
         def row_constants_1():
+            nc.tensor.transpose(lam_ps[:], lam_rows[:], ident_b[:])
+            nc.vector.tensor_copy(out=lam_c[:], in_=lam_ps[:, 0:NB])
             nc.gpsimd.tensor_tensor(out=rowk[:], in0=lam_c[:], in1=lam_c[:], op=ALU.mult)
             nc.gpsimd.tensor_scalar(
                 out=rowk[:], in0=rowk[:], scalar1=TINY * TINY, scalar2=2 * TINY, op0=ALU.is_lt, op1=ALU.mult
@@ -247,19 +258,25 @@ def tile_temporalaugmentedbilinear_w4_kernel(
         def product(i):
             v_sb = work.tile([NP, Q], F32, name="v_sb", bufs=8)
             vv[i] = v_sb
-            nc.vector.scalar_tensor_tensor(
-                out=v_sb[:], in0=ex[i][:], scalar=dr[i][:, i % 2, 0:1], in1=up[i][:], op0=ALU.add, op1=ALU.mult
-            )
+            for q in column_parts(i):
+                nc.vector.scalar_tensor_tensor(
+                    out=v_sb[:, q],
+                    in0=ex[i][:, q],
+                    scalar=dr[i][:, i % 2, 0:1],
+                    in1=up[i][:, q],
+                    op0=ALU.add,
+                    op1=ALU.mult,
+                )
 
         def row_coeff(i):
-            coeff = work.tile([NP, 2], F32, name="coeff", bufs=6)
+            coeff = work.tile([NP, 2], F32, name="coeff", bufs=8)
             cf[i], cf[i + 1] = coeff[:, 0:1], coeff[:, 1:2]
             nc.vector.reciprocal(out=coeff[:], in_=dr[i][:, :, 1])
 
         dg, bs = {}, {}
 
         def scale_bias(i):
-            b_sc = work.tile([NP, Q], F32, name="b_sc", bufs=3)
+            b_sc = work.tile([NP, Q], F32, name="b_sc", bufs=4)
             bs[i] = b_sc
             nc.gpsimd.tensor_scalar(
                 out=b_sc[:],
@@ -285,9 +302,15 @@ def tile_temporalaugmentedbilinear_w4_kernel(
         def add_bias_v(i):
             z_v = work.tile([NP, Q], F32, name="z_v", bufs=2)
             zz[i] = z_v
-            nc.vector.scalar_tensor_tensor(
-                out=z_v[:], in0=vv[i][:], scalar=cf[i], in1=bias_t[:, i % NB, :], op0=ALU.mult, op1=ALU.add
-            )
+            for q in column_parts(i):
+                nc.vector.scalar_tensor_tensor(
+                    out=z_v[:, q],
+                    in0=vv[i][:, q],
+                    scalar=cf[i],
+                    in1=bias_t[:, i % NB, q],
+                    op0=ALU.mult,
+                    op1=ALU.add,
+                )
 
         def bias_mm(i):
             z_ps = psum.tile([NP, Q], F32, name="z_ps", tag="z", bufs=1)
@@ -299,8 +322,9 @@ def tile_temporalaugmentedbilinear_w4_kernel(
             b, pb = divmod(i, NB)
             o_sb = work.tile([NP, Q], F32, name="o_sb", bufs=4)
             scale = cf[i] if kind(i) == "g" else 1.0
-            nc.scalar.activation(out=o_sb[:], in_=zz[i][:], func=ACT.Tanh, scale=scale)
-            nc.sync.dma_start(out=out[b, NP * pb : NP * (pb + 1), :], in_=o_sb[:])
+            for q in column_parts(i):
+                nc.scalar.activation(out=o_sb[:, q], in_=zz[i][:, q], func=ACT.Tanh, scale=scale)
+                nc.sync.dma_start(out=out[b, NP * pb : NP * (pb + 1), q], in_=o_sb[:, q])
 
         def valid(i):
             return 0 <= i < NT
@@ -308,61 +332,63 @@ def tile_temporalaugmentedbilinear_w4_kernel(
         def is_kind(i, k):
             return valid(i) and kind(i) == k
 
-        nc.tensor.transpose(lam_ps[:], lam_rows[:], ident_b[:])
         for s in range(4):
             widen(0, s)
-        nc.vector.tensor_copy(out=lam_c[:], in_=lam_ps[:, 0:NB])
         for c in range(4):
             interleave(0, c)
-        row_constants_1()
         quantise_x(0)
-        row_constants_2()
 
-        for n in range(-4, NT + 7):
-            b, c = divmod(n + 8, 4)
-            if 2 <= b < B:
-                interleave(b, c)
+        for n in range(-4, NT + 4):
             b, c = divmod(n + 4, 4)
             if 1 <= b < B and c == 0:
                 quantise_x(b)
-            if is_kind(n - 4, "g"):
-                add_bias(n - 4)
-            b, s = divmod(n + 12, 4)
-            if 2 <= b < B:
-                widen(b, s)
-            if valid(n + 4):
-                first_mm(n + 4)
             if valid(n):
                 row_max(n)
-            if valid(n):
-                exponent(n)
-            if is_kind(n - 4, "v"):
-                add_bias_v(n - 4)
-            if valid(n - 6):
-                finish(n - 6)
+            if is_kind(n - 4, "pe"):
+                make_diag(n - 4)
+            if is_kind(n - 3, "v"):
+                add_bias_v(n - 3)
+            if valid(n - 2):
+                product(n - 2)
             if n == -4:
                 for s in range(4):
                     widen(1, s)
             if n == -1:
                 for c in range(4):
                     interleave(1, c)
-            if valid(n - 2):
-                product(n - 2)
+            if valid(n + 4):
+                first_mm(n + 4)
+            if is_kind(n - 5, "pe"):
+                bias_mm(n - 5)
+            for i in range(n - 7, n):
+                if is_kind(i, "g") and i + (4 if i < TAIL else 3) == n:
+                    add_bias(i)
+            b, s = divmod(n + 12, 4)
+            if 2 <= b < B:
+                widen(b, s)
             if is_kind(n - 2, "g"):
                 scale_bias(n - 2)
-            if is_kind(n - 3, "pe"):
-                make_diag(n - 3)
             if n % 2 == 0 and valid(n + 2):
                 quantise_h(n // 2 + 1)
+            b, c = divmod(n + 8, 4)
+            if 2 <= b < B:
+                interleave(b, c)
+            if n == -3:
+                row_constants_1()
+            if n == -1:
+                row_constants_2()
+            if valid(n):
+                exponent(n)
+            for i in range(n - 9, n):
+                if valid(i) and finish_step(i) == n:
+                    finish(i)
             if n % 2 == 0 and valid(n - 2):
                 row_coeff(n - 2)
             if valid(n + 4):
                 apply_gain(n + 4)
-            if valid(n):
-                row_factors(n)
-            if is_kind(n - 5, "pe"):
-                bias_mm(n - 5)
             if valid(n - 1):
                 second_mm(n - 1, 2)
             if valid(n + 2):
                 second_mm(n + 2, 1)
+            if valid(n):
+                row_factors(n)

@@ -18,31 +18,33 @@ ALU = mybir.AluOpType
 ACT = mybir.ActivationFunctionType
 AX = mybir.AxisListType
 
-NP = 128
-NB = 4
-NT = B * NB
-TINY = 1e-15
+PARTS = 128
+PACK = 4
+ROW_TILES = P // PARTS
+TILES = B * ROW_TILES
+M_PART = PARTS // 4
+
+LAM_FLOOR = 1e-15
+
+WIDEN_ENGINES = ("vvvs", "ssss", "ssss")
+INTERLEAVE_ENGINES = ("vvvs", "ssgg", "ssgs")
+
+LAST_TILES = 24
+BIAS_ENGINES = "gpgvgpgg" * 3 + "gvgvgvvv"
 
 
-CHUNK_ENGINES = ("vvvs", "ssss", "sssg")
-WIDEN_ENGINES = ("vvvs", "svvv", "ssss")
-
-
-def column_parts(i):
-    return (slice(0, 256), slice(256, 512)) if i >= NT - 1 else (slice(0, 512),)
-
-
-KINDS = "gpgvgpgg"
-TAIL = 24
-TAIL_KINDS = "gvgvgvvv"
-
-
-def kind(i):
-    return {"p": "pe", "g": "g", "v": "v"}[TAIL_KINDS[i - TAIL] if i >= TAIL else KINDS[i % len(KINDS)]]
+def gpsimd_bias_step(i):
+    return i + (4 if i < LAST_TILES else 3)
 
 
 def finish_step(i):
-    return i + 5 - min(2, max(0, (i - 21) // 2))
+    return i + 5 - min(2, max(0, (i - LAST_TILES + 4) // 2))
+
+
+def column_parts(i):
+    if i == TILES - 1:
+        return (slice(0, Q // 2), slice(Q // 2, Q))
+    return (slice(0, Q),)
 
 
 def tile_temporalaugmentedbilinear_w4_kernel(
@@ -56,339 +58,347 @@ def tile_temporalaugmentedbilinear_w4_kernel(
         psum = ctx.enter_context(tc.psum_pool(name="psum", bufs=1))
         ctx.enter_context(tc.manual_schedule())
 
-        warm = keep.tile([NP, 1], F32, name="warm")
+        warm = keep.tile([PARTS, 1], F32, name="warm")
         nc.vector.memset(warm[:], 0.0)
-        warm_out = keep.tile([NP, 1], F32, name="warm_out")
+        warm_out = keep.tile([PARTS, 1], F32, name="warm_out")
         nc.scalar.activation(out=warm_out[:], in_=warm[:], func=ACT.Exp)
 
-        planes = keep.tile([NP, 3, P], U8, name="planes", align_bytes=64)
-        nc.vector.memset(planes[:].rearrange("p a n -> p (a n)").bitcast(I32), 0)
-        lam_rows = keep.tile([NP, NP], BF16, name="lam_rows")
+        weight_scales = keep.tile([PARTS, 3, P], U8, name="weight_scales", align_bytes=64)
+        nc.vector.memset(weight_scales[:].rearrange("p a n -> p (a n)").bitcast(I32), 0)
+        lam_rows = keep.tile([PARTS, PARTS], BF16, name="lam_rows")
         nc.vector.memset(lam_rows[:], 0.0)
 
-        ident_b = keep.tile([NP, NP], BF16, name="ident_b")
+        ident_b = keep.tile([PARTS, PARTS], BF16, name="ident_b")
         make_identity(nc, ident_b[:])
-        ident_f = keep.tile([NP, NP], F32, name="ident_f")
+        ident_f = keep.tile([PARTS, PARTS], F32, name="ident_f")
         make_identity(nc, ident_f[:])
 
-        xb = []
+        gain = keep.tile([PARTS, PACK], BF16, name="gain")
+        nc.gpsimd.dma_start(out=gain[:], in_=g.rearrange("(m j) -> m j", j=PACK))
+        nc.gpsimd.dma_start(out=lam_rows[0:ROW_TILES, :], in_=lam.rearrange("(r m) -> r m", m=PARTS))
+        bias_t = keep.tile([PARTS, ROW_TILES, Q], BF16, name="bias_t")
+        nc.gpsimd.dma_start(out=bias_t[:], in_=bias.rearrange("(r m) q -> m r q", m=PARTS))
+
+        x_codes_in = []
 
         def load_x(b):
-            codes_in = keep.tile([NP, 4, T], U8, name="codes_in%d" % b, align_bytes=64)
-            nc.sync.dma_start(out=codes_in[:], in_=x_bytes[b].rearrange("(p s) t -> p s t", s=4))
-            xb.append(codes_in)
+            x_in = keep.tile([PARTS, PACK, T], U8, name="x_in%d" % b, align_bytes=64)
+            nc.sync.dma_start(out=x_in[:], in_=x_bytes[b].rearrange("(p s) t -> p s t", s=PACK))
+            x_codes_in.append(x_in)
 
-        words = []
+        def load_words(words, name):
+            tile = keep.tile([PARTS, 2 * P], U8, name=name, align_bytes=64)
+            nc.sync.dma_start(out=tile[:].bitcast(I32), in_=words[0].bitcast(I32))
+            return tile
 
-        def load_words(src, name):
-            wt = keep.tile([NP, 2 * P], U8, name=name, align_bytes=64)
-            nc.sync.dma_start(out=wt[:].bitcast(I32), in_=src[0].bitcast(I32))
-            words.append(wt)
-
-        def load_plane(idx, src):
+        def load_scales(which, scales):
             for r in range(4):
                 nc.sync.dma_start(
-                    out=planes[r:NP:32, idx, :].bitcast(I32),
-                    in_=src[0, r:16:4, :].bitcast(I32),
+                    out=weight_scales[r:PARTS:32, which, :].bitcast(I32),
+                    in_=scales[0, r:16:4, :].bitcast(I32),
                 )
 
+        W1, W, W2 = 0, 1, 2
         load_x(0)
-        xs = keep.tile([NP, 4], F32, name="xs")
-        nc.sync.dma_start(out=xs[:], in_=x_scale.rearrange("o (p s) u -> p (o s u)", s=4))
-        load_words(w1_words, "w1_t")
-        load_plane(0, w1_scales)
+        feature_scale = keep.tile([PARTS, PACK], F32, name="feature_scale")
+        nc.sync.dma_start(out=feature_scale[:], in_=x_scale.rearrange("o (p s) u -> p (o s u)", s=PACK))
+        load_scales(W1, w1_scales)
+        w1_codes = load_words(w1_words, "w1_codes")
         load_x(1)
-        gain = keep.tile([NP, 4], BF16, name="gain")
-        nc.sync.dma_start(out=gain[:], in_=g.rearrange("(p j) -> p j", j=4))
-        load_words(w_words, "w_t")
-        load_plane(1, w_scales)
-        nc.sync.dma_start(out=lam_rows[0:NB, :], in_=lam.rearrange("(c p) -> c p", p=NP))
-        load_words(w2_words, "w2_t")
-        load_plane(2, w2_scales)
+        w_codes = load_words(w_words, "w_codes")
+        load_scales(W, w_scales)
         load_x(2)
-        bias_t = keep.tile([NP, NB, Q], BF16, name="bias_t")
-        nc.sync.dma_start(out=bias_t[:], in_=bias.rearrange("(c p) q -> p c q", p=NP))
+        w2_codes = load_words(w2_words, "w2_codes")
+        load_scales(W2, w2_scales)
         for b in range(3, B):
             load_x(b)
-        w1_t, w_t, w2_t = words
 
-        lam_c = keep.tile([NP, NB], F32, name="lam_c")
-        cst = keep.tile([NP, NB, 2], F32, name="cst")
+        lam_col = keep.tile([PARTS, ROW_TILES], F32, name="lam_col")
+        lam_tmp = keep.tile([PARTS, ROW_TILES], F32, name="lam_tmp")
+        row_const = keep.tile([PARTS, ROW_TILES, 2], F32, name="row_const")
+        lam_ps = psum.tile([PARTS, PARTS], BF16, name="lam_ps", tag="z_ps", bufs=1)
 
-        rowk = keep.tile([NP, NB], F32, name="rowk")
-        lam_ps = psum.tile([NP, NP], BF16, name="lam_ps", tag="z", bufs=1)
-
-        def row_constants_1():
+        def row_constants_first():
             nc.tensor.transpose(lam_ps[:], lam_rows[:], ident_b[:])
-            nc.vector.tensor_copy(out=lam_c[:], in_=lam_ps[:, 0:NB])
-            nc.gpsimd.tensor_tensor(out=rowk[:], in0=lam_c[:], in1=lam_c[:], op=ALU.mult)
+            nc.vector.tensor_copy(out=lam_col[:], in_=lam_ps[:, 0:ROW_TILES])
+            nc.gpsimd.tensor_tensor(out=lam_tmp[:], in0=lam_col[:], in1=lam_col[:], op=ALU.mult)
             nc.gpsimd.tensor_scalar(
-                out=rowk[:], in0=rowk[:], scalar1=TINY * TINY, scalar2=2 * TINY, op0=ALU.is_lt, op1=ALU.mult
+                out=lam_tmp[:],
+                in0=lam_tmp[:],
+                scalar1=LAM_FLOOR * LAM_FLOOR,
+                scalar2=2 * LAM_FLOOR,
+                op0=ALU.is_lt,
+                op1=ALU.mult,
             )
-            nc.gpsimd.tensor_tensor(out=rowk[:], in0=rowk[:], in1=lam_c[:], op=ALU.add)
+            nc.gpsimd.tensor_tensor(out=lam_tmp[:], in0=lam_tmp[:], in1=lam_col[:], op=ALU.add)
             nc.gpsimd.tensor_scalar(
-                out=rowk[:], in0=rowk[:], scalar1=float(Q), scalar2=0.0, op0=ALU.mult, op1=ALU.add
+                out=lam_tmp[:], in0=lam_tmp[:], scalar1=float(Q), scalar2=0.0, op0=ALU.mult, op1=ALU.add
             )
             nc.gpsimd.tensor_scalar(
-                out=lam_c[:], in0=lam_c[:], scalar1=-1.0, scalar2=1.0, op0=ALU.mult, op1=ALU.add
+                out=lam_col[:], in0=lam_col[:], scalar1=-1.0, scalar2=1.0, op0=ALU.mult, op1=ALU.add
             )
 
-        def row_constants_2():
-            nc.vector.reciprocal(out=cst[:, :, 1], in_=rowk[:])
-            nc.gpsimd.tensor_tensor(out=cst[:, :, 0], in0=lam_c[:], in1=cst[:, :, 1], op=ALU.mult)
+        def row_constants_second():
+            nc.vector.reciprocal(out=row_const[:, :, 1], in_=lam_tmp[:])
+            nc.gpsimd.tensor_tensor(out=row_const[:, :, 0], in0=lam_col[:], in1=row_const[:, :, 1], op=ALU.mult)
 
-        xw, xg, xq, xqs = {}, {}, {}, {}
+        x_wide, x_grouped, x_codes, x_scales = {}, {}, {}, {}
 
         def widen(b, s):
             if s == 0:
-                wide = work.tile([NP, 4, T], BF16, name="wide", bufs=3, align_bytes=64)
-                xw[b] = wide
-            src = xb[b][:, s, :].bitcast(FP8)
+                wide = work.tile([PARTS, PACK, T], BF16, name="wide", bufs=3, align_bytes=64)
+                x_wide[b] = wide
+            src = x_codes_in[b][:, s, :].bitcast(FP8)
+            dst = x_wide[b][:, s, :]
+            scale = feature_scale[:, s : s + 1]
             if WIDEN_ENGINES[min(b, 2)][s] == "v":
-                nc.vector.tensor_scalar(
-                    out=xw[b][:, s, :], in0=src, scalar1=xs[:, s : s + 1], scalar2=None, op0=ALU.mult
-                )
+                nc.vector.tensor_scalar(out=dst, in0=src, scalar1=scale, scalar2=None, op0=ALU.mult)
             else:
-                nc.scalar.activation(out=xw[b][:, s, :], in_=src, func=ACT.Copy, scale=xs[:, s : s + 1])
+                nc.scalar.activation(out=dst, in_=src, func=ACT.Copy, scale=scale)
 
         def interleave(b, c):
             if c == 0:
-                grouped_x = work.tile([NP, 4, NP, 4], BF16, name="grouped_x", bufs=3, align_bytes=64)
-                xg[b] = grouped_x
-            o = xg[b][:, :, 32 * c : 32 * c + 32, :].rearrange("p j m s -> p m j s")
-            i = xw[b][:, :, NP * c : NP * c + NP].rearrange("p s (m j) -> p m j s", j=4)
-            eng = CHUNK_ENGINES[min(b, 2)][c]
-            if eng == "v":
-                nc.vector.tensor_copy(out=o, in_=i)
-            elif eng == "s":
-                nc.scalar.copy(out=o, in_=i)
+                grouped = work.tile([PARTS, PACK, PARTS, PACK], BF16, name="grouped", bufs=3, align_bytes=64)
+                x_grouped[b] = grouped
+            dst = x_grouped[b][:, :, M_PART * c : M_PART * (c + 1), :].rearrange("p j m s -> p m j s")
+            src = x_wide[b][:, :, PARTS * c : PARTS * (c + 1)].rearrange("p s (m j) -> p m j s", j=PACK)
+            engine = INTERLEAVE_ENGINES[min(b, 2)][c]
+            if engine == "v":
+                nc.vector.tensor_copy(out=dst, in_=src)
+            elif engine == "s":
+                nc.scalar.copy(out=dst, in_=src)
             else:
-                nc.gpsimd.tensor_scalar(out=o, in0=i, scalar1=1.0, scalar2=0.0, op0=ALU.mult, op1=ALU.add)
+                nc.gpsimd.tensor_scalar(out=dst, in0=src, scalar1=1.0, scalar2=0.0, op0=ALU.mult, op1=ALU.add)
 
         def quantise_x(b):
-            x_codes = work.tile([NP, T], U32, name="x_codes", bufs=2, align_bytes=64)
-            x_plane = work.tile([NP, T], U8, name="x_plane", bufs=2, align_bytes=64)
+            codes = work.tile([PARTS, T], U32, name="xq_codes", bufs=2, align_bytes=64)
+            scales = work.tile([PARTS, T], U8, name="xq_scales", bufs=2, align_bytes=64)
             nc.vector.quantize_mx(
-                out=x_codes[:].bitcast(FP8X4),
-                scales=x_plane[:],
-                in_=xg[b][:].rearrange("p j m s -> p (j m s)"),
+                out=codes[:].bitcast(FP8X4),
+                scales=scales[:],
+                in_=x_grouped[b][:].rearrange("p j m s -> p (j m s)"),
             )
-            xq[b], xqs[b] = x_codes, x_plane
+            x_codes[b], x_scales[b] = codes, scales
 
-        hp, hg, hq, hqs = {}, {}, {}, {}
+        h0, h_grouped, h_codes, h_scales = {}, {}, {}, {}
 
-        def first_mm(i):
-            b, pb = divmod(i, NB)
-            h_ps = psum.tile([NP, 4, NP], F32, name="h_ps", bufs=2)
-            hp[i] = h_ps
-            for j in range(4):
+        def first_matmul(i):
+            b, r = divmod(i, ROW_TILES)
+            h_ps = psum.tile([PARTS, PACK, PARTS], F32, name="h_ps", bufs=2)
+            h0[i] = h_ps
+            for j in range(PACK):
+                cols = slice(PARTS * j, PARTS * (j + 1))
                 nc.tensor.matmul_mx(
                     out=h_ps[:, j, :],
-                    lhsT=xq[b][:, NP * j : NP * j + NP].bitcast(FP8X4),
-                    lhsT_scale=xqs[b][:, NP * j : NP * j + NP],
-                    rhs=w1_t[:, 2 * NP * pb : 2 * NP * (pb + 1)].bitcast(FP4X4),
-                    rhs_scale=planes[:, 0, NP * pb : NP * (pb + 1)],
+                    lhsT=x_codes[b][:, cols].bitcast(FP8X4),
+                    lhsT_scale=x_scales[b][:, cols],
+                    rhs=w1_codes[:, 2 * PARTS * r : 2 * PARTS * (r + 1)].bitcast(FP4X4),
+                    rhs_scale=weight_scales[:, W1, PARTS * r : PARTS * (r + 1)],
                     start=True,
                     stop=True,
                 )
 
         def apply_gain(i):
             if i % 2 == 0:
-                grouped_h = work.tile([NP, 2, NP, 4], BF16, name="grouped_h", bufs=2, align_bytes=64)
-                hg[i // 2] = grouped_h
+                h_pair = work.tile([PARTS, 2, PARTS, PACK], BF16, name="h_pair", bufs=2, align_bytes=64)
+                h_grouped[i // 2] = h_pair
             nc.vector.tensor_tensor(
-                out=hg[i // 2][:, i % 2, :, :],
-                in0=hp[i][:].rearrange("p j n -> p n j"),
-                in1=gain[:].unsqueeze(1).to_broadcast([NP, NP, 4]),
+                out=h_grouped[i // 2][:, i % 2, :, :],
+                in0=h0[i][:].rearrange("m j n -> m n j"),
+                in1=gain[:].unsqueeze(1).to_broadcast([PARTS, PARTS, PACK]),
                 op=ALU.mult,
             )
 
-        def quantise_h(i):
-            h_codes = work.tile([NP, 2 * NP], U32, name="h_codes", bufs=3, align_bytes=64)
-            h_plane = work.tile([NP, 2 * NP], U8, name="h_plane", bufs=3, align_bytes=64)
+        def quantise_h(pair):
+            codes = work.tile([PARTS, 2 * PARTS], U32, name="hq_codes", bufs=3, align_bytes=64)
+            scales = work.tile([PARTS, 2 * PARTS], U8, name="hq_scales", bufs=3, align_bytes=64)
             nc.vector.quantize_mx(
-                out=h_codes[:].bitcast(FP8X4),
-                scales=h_plane[:],
-                in_=hg[i][:].rearrange("p u n j -> p (u n j)"),
+                out=codes[:].bitcast(FP8X4),
+                scales=scales[:],
+                in_=h_grouped[pair][:].rearrange("m a n j -> m (a n j)"),
             )
-            hq[i], hqs[i] = h_codes, h_plane
+            h_codes[pair], h_scales[pair] = codes, scales
 
-        ep, up = {}, {}
+        e_of, u_of = {}, {}
 
-        def second_mm(i, which):
-            if which == 1:
-                e_ps = psum.tile([NP, Q], F32, name="e_ps", bufs=3)
-                ep[i] = e_ps
-                dst, wt = e_ps, w_t
-            else:
-                u_ps = psum.tile([NP, Q], F32, name="u_ps", bufs=2)
-                up[i] = u_ps
-                dst, wt = u_ps, w2_t
+        def second_matmul(i, dst, codes, which):
+            cols = slice(PARTS * (i % 2), PARTS * (i % 2 + 1))
             nc.tensor.matmul_mx(
                 out=dst[:],
-                lhsT=hq[i // 2][:, NP * (i % 2) : NP * (i % 2) + NP].bitcast(FP8X4),
-                lhsT_scale=hqs[i // 2][:, NP * (i % 2) : NP * (i % 2) + NP],
-                rhs=wt[:].bitcast(FP4X4),
-                rhs_scale=planes[:, which, :],
+                lhsT=h_codes[i // 2][:, cols].bitcast(FP8X4),
+                lhsT_scale=h_scales[i // 2][:, cols],
+                rhs=codes[:].bitcast(FP4X4),
+                rhs_scale=weight_scales[:, which, :],
                 start=True,
                 stop=True,
             )
 
-        nmax, ex, sm, dr, cf, vv, zz, ot = {}, {}, {}, {}, {}, {}, {}, {}
+        def scores(i):
+            e_ps = psum.tile([PARTS, Q], F32, name="e_ps", bufs=3)
+            e_of[i] = e_ps
+            second_matmul(i, e_ps, w_codes, W)
+
+        def mode(i):
+            u_ps = psum.tile([PARTS, Q], F32, name="u_ps", bufs=2)
+            u_of[i] = u_ps
+            second_matmul(i, u_ps, w2_codes, W2)
+
+        neg_max, exps, sums, factors, coeff = {}, {}, {}, {}, {}
+        mixed, scaled_bias, diags, z_of = {}, {}, {}, {}
 
         def row_max(i):
-            neg_max = work.tile([NP, 1], F32, name="neg_max", bufs=4)
-            nmax[i] = neg_max
-            nc.vector.tensor_reduce(out=neg_max[:], in_=ep[i][:], axis=AX.X, op=ALU.max, negate=True)
+            nmax = work.tile([PARTS, 1], F32, name="nmax", bufs=4)
+            neg_max[i] = nmax
+            nc.vector.tensor_reduce(out=nmax[:], in_=e_of[i][:], axis=AX.X, op=ALU.max, negate=True)
 
-        def exponent(i):
-            e_sb = work.tile([NP, Q], F32, name="e_sb", bufs=4)
-            e_sum = work.tile([NP, 1], F32, name="e_sum", bufs=10)
-            ex[i], sm[i] = e_sb, e_sum
+        def exponentials(i):
+            e_sb = work.tile([PARTS, Q], F32, name="e_sb", bufs=4)
+            e_sum = work.tile([PARTS, 1], F32, name="e_sum", bufs=10)
+            exps[i], sums[i] = e_sb, e_sum
             nc.scalar.activation(
-                out=e_sb[:], in_=ep[i][:], func=ACT.Exp, bias=nmax[i][:], scale=1.0, accum_out=e_sum[:]
+                out=e_sb[:], in_=e_of[i][:], func=ACT.Exp, bias=neg_max[i][:], scale=1.0, accum_out=e_sum[:]
             )
 
         def row_factors(i):
             if i % 2 == 0:
-                d_rc = work.tile([NP, 2, 2], F32, name="d_rc", bufs=6)
-                dr[i] = dr[i + 1] = d_rc
-            nc.scalar.activation(out=dr[i][:, i % 2, :], in_=cst[:, i % NB, :], func=ACT.Copy, scale=sm[i][:])
+                pair = work.tile([PARTS, 2, 2], F32, name="pair", bufs=6)
+                factors[i] = factors[i + 1] = pair
+            nc.scalar.activation(
+                out=factors[i][:, i % 2, :], in_=row_const[:, i % ROW_TILES, :], func=ACT.Copy, scale=sums[i][:]
+            )
 
-        def product(i):
-            v_sb = work.tile([NP, Q], F32, name="v_sb", bufs=8)
-            vv[i] = v_sb
+        def row_coefficients(i):
+            inverse = work.tile([PARTS, 2], F32, name="inverse", bufs=8)
+            coeff[i], coeff[i + 1] = inverse[:, 0:1], inverse[:, 1:2]
+            nc.vector.reciprocal(out=inverse[:], in_=factors[i][:, :, 1])
+
+        def mix(i):
+            v_sb = work.tile([PARTS, Q], F32, name="v_sb", bufs=8)
+            mixed[i] = v_sb
             for q in column_parts(i):
                 nc.vector.scalar_tensor_tensor(
                     out=v_sb[:, q],
-                    in0=ex[i][:, q],
-                    scalar=dr[i][:, i % 2, 0:1],
-                    in1=up[i][:, q],
+                    in0=exps[i][:, q],
+                    scalar=factors[i][:, i % 2, 0:1],
+                    in1=u_of[i][:, q],
                     op0=ALU.add,
                     op1=ALU.mult,
                 )
 
-        def row_coeff(i):
-            coeff = work.tile([NP, 2], F32, name="coeff", bufs=8)
-            cf[i], cf[i + 1] = coeff[:, 0:1], coeff[:, 1:2]
-            nc.vector.reciprocal(out=coeff[:], in_=dr[i][:, :, 1])
-
-        dg, bs = {}, {}
+        def bias_on_vector(i):
+            z_v = work.tile([PARTS, Q], F32, name="z_v", bufs=2)
+            z_of[i] = z_v
+            for q in column_parts(i):
+                nc.vector.scalar_tensor_tensor(
+                    out=z_v[:, q],
+                    in0=mixed[i][:, q],
+                    scalar=coeff[i],
+                    in1=bias_t[:, i % ROW_TILES, q],
+                    op0=ALU.mult,
+                    op1=ALU.add,
+                )
 
         def scale_bias(i):
-            b_sc = work.tile([NP, Q], F32, name="b_sc", bufs=4)
-            bs[i] = b_sc
+            bias_ys = work.tile([PARTS, Q], F32, name="bias_ys", bufs=4)
+            scaled_bias[i] = bias_ys
             nc.gpsimd.tensor_scalar(
-                out=b_sc[:],
-                in0=bias_t[:, i % NB, :],
-                scalar1=dr[i][:, i % 2, 1:2],
+                out=bias_ys[:],
+                in0=bias_t[:, i % ROW_TILES, :],
+                scalar1=factors[i][:, i % 2, 1:2],
                 scalar2=0.0,
                 op0=ALU.mult,
                 op1=ALU.add,
             )
 
-        def add_bias(i):
-            z_sb = work.tile([NP, Q], F32, name="z_sb", bufs=3)
-            zz[i] = z_sb
-            nc.gpsimd.tensor_tensor(out=z_sb[:], in0=vv[i][:], in1=bs[i][:], op=ALU.add)
+        def bias_on_gpsimd(i):
+            z_g = work.tile([PARTS, Q], F32, name="z_g", bufs=3)
+            z_of[i] = z_g
+            nc.gpsimd.tensor_tensor(out=z_g[:], in0=mixed[i][:], in1=scaled_bias[i][:], op=ALU.add)
 
-        def make_diag(i):
-            diag = work.tile([NP, NP], F32, name="diag", bufs=3)
-            dg[i] = diag
+        def make_diagonal(i):
+            diag = work.tile([PARTS, PARTS], F32, name="diag", bufs=3)
+            diags[i] = diag
             nc.gpsimd.tensor_scalar(
-                out=diag[:], in0=ident_f[:], scalar1=cf[i], scalar2=0.0, op0=ALU.mult, op1=ALU.add
+                out=diag[:], in0=ident_f[:], scalar1=coeff[i], scalar2=0.0, op0=ALU.mult, op1=ALU.add
             )
 
-        def add_bias_v(i):
-            z_v = work.tile([NP, Q], F32, name="z_v", bufs=2)
-            zz[i] = z_v
-            for q in column_parts(i):
-                nc.vector.scalar_tensor_tensor(
-                    out=z_v[:, q],
-                    in0=vv[i][:, q],
-                    scalar=cf[i],
-                    in1=bias_t[:, i % NB, q],
-                    op0=ALU.mult,
-                    op1=ALU.add,
-                )
-
-        def bias_mm(i):
-            z_ps = psum.tile([NP, Q], F32, name="z_ps", tag="z", bufs=1)
-            zz[i] = z_ps
-            nc.tensor.matmul(z_ps[:], lhsT=ident_b[:], rhs=bias_t[:, i % NB, :], start=True, stop=False)
-            nc.tensor.matmul(z_ps[:], lhsT=dg[i][:], rhs=vv[i][:], start=False, stop=True)
+        def bias_on_tensor(i):
+            z_ps = psum.tile([PARTS, Q], F32, name="z_ps", bufs=1)
+            z_of[i] = z_ps
+            nc.tensor.matmul(z_ps[:], lhsT=ident_b[:], rhs=bias_t[:, i % ROW_TILES, :], start=True, stop=False)
+            nc.tensor.matmul(z_ps[:], lhsT=diags[i][:], rhs=mixed[i][:], start=False, stop=True)
 
         def finish(i):
-            b, pb = divmod(i, NB)
-            o_sb = work.tile([NP, Q], F32, name="o_sb", bufs=4)
-            scale = cf[i] if kind(i) == "g" else 1.0
+            b, r = divmod(i, ROW_TILES)
+            result = work.tile([PARTS, Q], F32, name="result", bufs=4)
+            scale = coeff[i] if BIAS_ENGINES[i] == "g" else 1.0
             for q in column_parts(i):
-                nc.scalar.activation(out=o_sb[:, q], in_=zz[i][:, q], func=ACT.Tanh, scale=scale)
-                nc.sync.dma_start(out=out[b, NP * pb : NP * (pb + 1), q], in_=o_sb[:, q])
+                nc.scalar.activation(out=result[:, q], in_=z_of[i][:, q], func=ACT.Tanh, scale=scale)
+                nc.sync.dma_start(out=out[b, PARTS * r : PARTS * (r + 1), q], in_=result[:, q])
 
-        def valid(i):
-            return 0 <= i < NT
+        def is_tile(i):
+            return 0 <= i < TILES
 
-        def is_kind(i, k):
-            return valid(i) and kind(i) == k
+        def has_bias_on(i, engine):
+            return is_tile(i) and BIAS_ENGINES[i] == engine
 
-        for s in range(4):
+        for s in range(PACK):
             widen(0, s)
         for c in range(4):
             interleave(0, c)
         quantise_x(0)
 
-        for n in range(-4, NT + 4):
-            b, c = divmod(n + 4, 4)
-            if 1 <= b < B and c == 0:
-                quantise_x(b)
-            if valid(n):
+        for n in range(-4, finish_step(TILES - 1) + 1):
+            quantise_batch, quantise_phase = divmod(n + 4, 4)
+            interleave_batch, interleave_part = divmod(n + 8, 4)
+            widen_batch, widen_slot = divmod(n + 12, 4)
+
+            if 1 <= quantise_batch < B and quantise_phase == 0:
+                quantise_x(quantise_batch)
+            if is_tile(n):
                 row_max(n)
-            if is_kind(n - 4, "pe"):
-                make_diag(n - 4)
-            if is_kind(n - 3, "v"):
-                add_bias_v(n - 3)
-            if valid(n - 2):
-                product(n - 2)
+            for i in (n - 4, n - 3):
+                if has_bias_on(i, "g") and gpsimd_bias_step(i) == n:
+                    bias_on_gpsimd(i)
+            if has_bias_on(n - 5, "p"):
+                make_diagonal(n - 5)
+            if n == -2:
+                row_constants_first()
+            if n == 0:
+                row_constants_second()
+            if has_bias_on(n - 3, "v"):
+                bias_on_vector(n - 3)
+            if is_tile(n - 2):
+                mix(n - 2)
+            if 2 <= interleave_batch < B:
+                interleave(interleave_batch, interleave_part)
             if n == -4:
-                for s in range(4):
+                for s in range(PACK):
                     widen(1, s)
-            if n == -1:
                 for c in range(4):
                     interleave(1, c)
-            if valid(n + 4):
-                first_mm(n + 4)
-            if is_kind(n - 5, "pe"):
-                bias_mm(n - 5)
-            for i in range(n - 7, n):
-                if is_kind(i, "g") and i + (4 if i < TAIL else 3) == n:
-                    add_bias(i)
-            b, s = divmod(n + 12, 4)
-            if 2 <= b < B:
-                widen(b, s)
-            if is_kind(n - 2, "g"):
+            if is_tile(n + 4):
+                first_matmul(n + 4)
+            if is_tile(n):
+                exponentials(n)
+            if has_bias_on(n - 5, "p"):
+                bias_on_tensor(n - 5)
+            if 2 <= widen_batch < B:
+                widen(widen_batch, widen_slot)
+            if is_tile(n - 1):
+                mode(n - 1)
+            if has_bias_on(n - 2, "g"):
                 scale_bias(n - 2)
-            if n % 2 == 0 and valid(n + 2):
-                quantise_h(n // 2 + 1)
-            b, c = divmod(n + 8, 4)
-            if 2 <= b < B:
-                interleave(b, c)
-            if n == -3:
-                row_constants_1()
-            if n == -1:
-                row_constants_2()
-            if valid(n):
-                exponent(n)
-            for i in range(n - 9, n):
-                if valid(i) and finish_step(i) == n:
-                    finish(i)
-            if n % 2 == 0 and valid(n - 2):
-                row_coeff(n - 2)
-            if valid(n + 4):
-                apply_gain(n + 4)
-            if valid(n - 1):
-                second_mm(n - 1, 2)
-            if valid(n + 2):
-                second_mm(n + 2, 1)
-            if valid(n):
+            if n % 2 == 0 and is_tile(n + 2):
+                quantise_h((n + 2) // 2)
+            if is_tile(n):
                 row_factors(n)
+            if is_tile(n + 2):
+                scores(n + 2)
+            if is_tile(n + 4):
+                apply_gain(n + 4)
+            for i in range(n - 5, n - 2):
+                if is_tile(i) and finish_step(i) == n:
+                    finish(i)
+            if n % 2 == 0 and is_tile(n - 2):
+                row_coefficients(n - 2)

from contextlib import ExitStack

import concourse.mybir as mybir
from concourse.masks import make_identity

B, D, T, P, Q = 8, 512, 512, 512, 512
FLOPS = 3 * 2 * B * D * T * P

F32 = mybir.dt.float32
BF16 = mybir.dt.bfloat16
U32 = mybir.dt.uint32
I32 = mybir.dt.int32
U8 = mybir.dt.uint8
FP8 = mybir.dt.float8_e4m3fn
FP8X4 = mybir.dt.float8_e4m3fn_x4
FP4X4 = mybir.dt.float4_e2m1fn_x4
ALU = mybir.AluOpType
ACT = mybir.ActivationFunctionType
AX = mybir.AxisListType

PARTS = 128
PACK = 4
ROW_TILES = P // PARTS
TILES = B * ROW_TILES
M_PART = PARTS // 4

LAM_FLOOR = 1e-15

WIDEN_ENGINES = ("vvvs", "ssss", "ssss")
INTERLEAVE_ENGINES = ("vvvs", "ssgg", "ssgs")

LAST_TILES = 24
BIAS_ENGINES = "gpgvgpgg" * 3 + "gvgvgvvv"


def gpsimd_bias_step(i):
    return i + (4 if i < LAST_TILES else 3)


def finish_step(i):
    return i + 5 - min(2, max(0, (i - LAST_TILES + 4) // 2))


def column_parts(i):
    if i == TILES - 1:
        return (slice(0, Q // 2), slice(Q // 2, Q))
    return (slice(0, Q),)


def tile_temporalaugmentedbilinear_w4_kernel(
    tc, x_bytes, x_scale, w1_words, w1_scales, g, w_words, w_scales, w2_words, w2_scales, lam, bias, out
):
    nc = tc.nc

    with ExitStack() as ctx:
        keep = ctx.enter_context(tc.tile_pool(name="keep", bufs=1))
        work = ctx.enter_context(tc.tile_pool(name="work", bufs=2))
        psum = ctx.enter_context(tc.psum_pool(name="psum", bufs=1))
        ctx.enter_context(tc.manual_schedule())

        warm = keep.tile([PARTS, 1], F32, name="warm")
        nc.vector.memset(warm[:], 0.0)
        warm_out = keep.tile([PARTS, 1], F32, name="warm_out")
        nc.scalar.activation(out=warm_out[:], in_=warm[:], func=ACT.Exp)

        weight_scales = keep.tile([PARTS, 3, P], U8, name="weight_scales", align_bytes=64)
        nc.vector.memset(weight_scales[:].rearrange("p a n -> p (a n)").bitcast(I32), 0)
        lam_rows = keep.tile([PARTS, PARTS], BF16, name="lam_rows")
        nc.vector.memset(lam_rows[:], 0.0)

        ident_b = keep.tile([PARTS, PARTS], BF16, name="ident_b")
        make_identity(nc, ident_b[:])
        ident_f = keep.tile([PARTS, PARTS], F32, name="ident_f")
        make_identity(nc, ident_f[:])

        gain = keep.tile([PARTS, PACK], BF16, name="gain")
        nc.gpsimd.dma_start(out=gain[:], in_=g.rearrange("(m j) -> m j", j=PACK))
        nc.gpsimd.dma_start(out=lam_rows[0:ROW_TILES, :], in_=lam.rearrange("(r m) -> r m", m=PARTS))
        bias_t = keep.tile([PARTS, ROW_TILES, Q], BF16, name="bias_t")
        nc.gpsimd.dma_start(out=bias_t[:], in_=bias.rearrange("(r m) q -> m r q", m=PARTS))

        x_codes_in = []

        def load_x(b):
            x_in = keep.tile([PARTS, PACK, T], U8, name="x_in%d" % b, align_bytes=64)
            nc.sync.dma_start(out=x_in[:], in_=x_bytes[b].rearrange("(p s) t -> p s t", s=PACK))
            x_codes_in.append(x_in)

        def load_words(words, name):
            tile = keep.tile([PARTS, 2 * P], U8, name=name, align_bytes=64)
            nc.sync.dma_start(out=tile[:].bitcast(I32), in_=words[0].bitcast(I32))
            return tile

        def load_scales(which, scales):
            for r in range(4):
                nc.sync.dma_start(
                    out=weight_scales[r:PARTS:32, which, :].bitcast(I32),
                    in_=scales[0, r:16:4, :].bitcast(I32),
                )

        W1, W, W2 = 0, 1, 2
        load_x(0)
        feature_scale = keep.tile([PARTS, PACK], F32, name="feature_scale")
        nc.sync.dma_start(out=feature_scale[:], in_=x_scale.rearrange("o (p s) u -> p (o s u)", s=PACK))
        load_scales(W1, w1_scales)
        w1_codes = load_words(w1_words, "w1_codes")
        load_x(1)
        w_codes = load_words(w_words, "w_codes")
        load_scales(W, w_scales)
        load_x(2)
        w2_codes = load_words(w2_words, "w2_codes")
        load_scales(W2, w2_scales)
        for b in range(3, B):
            load_x(b)

        lam_col = keep.tile([PARTS, ROW_TILES], F32, name="lam_col")
        lam_tmp = keep.tile([PARTS, ROW_TILES], F32, name="lam_tmp")
        row_const = keep.tile([PARTS, ROW_TILES, 2], F32, name="row_const")
        lam_ps = psum.tile([PARTS, PARTS], BF16, name="lam_ps", tag="z_ps", bufs=1)

        def row_constants_first():
            nc.tensor.transpose(lam_ps[:], lam_rows[:], ident_b[:])
            nc.vector.tensor_copy(out=lam_col[:], in_=lam_ps[:, 0:ROW_TILES])
            nc.gpsimd.tensor_tensor(out=lam_tmp[:], in0=lam_col[:], in1=lam_col[:], op=ALU.mult)
            nc.gpsimd.tensor_scalar(
                out=lam_tmp[:],
                in0=lam_tmp[:],
                scalar1=LAM_FLOOR * LAM_FLOOR,
                scalar2=2 * LAM_FLOOR,
                op0=ALU.is_lt,
                op1=ALU.mult,
            )
            nc.gpsimd.tensor_tensor(out=lam_tmp[:], in0=lam_tmp[:], in1=lam_col[:], op=ALU.add)
            nc.gpsimd.tensor_scalar(
                out=lam_tmp[:], in0=lam_tmp[:], scalar1=float(Q), scalar2=0.0, op0=ALU.mult, op1=ALU.add
            )
            nc.gpsimd.tensor_scalar(
                out=lam_col[:], in0=lam_col[:], scalar1=-1.0, scalar2=1.0, op0=ALU.mult, op1=ALU.add
            )

        def row_constants_second():
            nc.vector.reciprocal(out=row_const[:, :, 1], in_=lam_tmp[:])
            nc.gpsimd.tensor_tensor(out=row_const[:, :, 0], in0=lam_col[:], in1=row_const[:, :, 1], op=ALU.mult)

        x_wide, x_grouped, x_codes, x_scales = {}, {}, {}, {}

        def widen(b, s):
            if s == 0:
                wide = work.tile([PARTS, PACK, T], BF16, name="wide", bufs=3, align_bytes=64)
                x_wide[b] = wide
            src = x_codes_in[b][:, s, :].bitcast(FP8)
            dst = x_wide[b][:, s, :]
            scale = feature_scale[:, s : s + 1]
            if WIDEN_ENGINES[min(b, 2)][s] == "v":
                nc.vector.tensor_scalar(out=dst, in0=src, scalar1=scale, scalar2=None, op0=ALU.mult)
            else:
                nc.scalar.activation(out=dst, in_=src, func=ACT.Copy, scale=scale)

        def interleave(b, c):
            if c == 0:
                grouped = work.tile([PARTS, PACK, PARTS, PACK], BF16, name="grouped", bufs=3, align_bytes=64)
                x_grouped[b] = grouped
            dst = x_grouped[b][:, :, M_PART * c : M_PART * (c + 1), :].rearrange("p j m s -> p m j s")
            src = x_wide[b][:, :, PARTS * c : PARTS * (c + 1)].rearrange("p s (m j) -> p m j s", j=PACK)
            engine = INTERLEAVE_ENGINES[min(b, 2)][c]
            if engine == "v":
                nc.vector.tensor_copy(out=dst, in_=src)
            elif engine == "s":
                nc.scalar.copy(out=dst, in_=src)
            else:
                nc.gpsimd.tensor_scalar(out=dst, in0=src, scalar1=1.0, scalar2=0.0, op0=ALU.mult, op1=ALU.add)

        def quantise_x(b):
            codes = work.tile([PARTS, T], U32, name="xq_codes", bufs=2, align_bytes=64)
            scales = work.tile([PARTS, T], U8, name="xq_scales", bufs=2, align_bytes=64)
            nc.vector.quantize_mx(
                out=codes[:].bitcast(FP8X4),
                scales=scales[:],
                in_=x_grouped[b][:].rearrange("p j m s -> p (j m s)"),
            )
            x_codes[b], x_scales[b] = codes, scales

        h0, h_grouped, h_codes, h_scales = {}, {}, {}, {}

        def first_matmul(i):
            b, r = divmod(i, ROW_TILES)
            h_ps = psum.tile([PARTS, PACK, PARTS], F32, name="h_ps", bufs=2)
            h0[i] = h_ps
            for j in range(PACK):
                cols = slice(PARTS * j, PARTS * (j + 1))
                nc.tensor.matmul_mx(
                    out=h_ps[:, j, :],
                    lhsT=x_codes[b][:, cols].bitcast(FP8X4),
                    lhsT_scale=x_scales[b][:, cols],
                    rhs=w1_codes[:, 2 * PARTS * r : 2 * PARTS * (r + 1)].bitcast(FP4X4),
                    rhs_scale=weight_scales[:, W1, PARTS * r : PARTS * (r + 1)],
                    start=True,
                    stop=True,
                )

        def apply_gain(i):
            if i % 2 == 0:
                h_pair = work.tile([PARTS, 2, PARTS, PACK], BF16, name="h_pair", bufs=2, align_bytes=64)
                h_grouped[i // 2] = h_pair
            nc.vector.tensor_tensor(
                out=h_grouped[i // 2][:, i % 2, :, :],
                in0=h0[i][:].rearrange("m j n -> m n j"),
                in1=gain[:].unsqueeze(1).to_broadcast([PARTS, PARTS, PACK]),
                op=ALU.mult,
            )

        def quantise_h(pair):
            codes = work.tile([PARTS, 2 * PARTS], U32, name="hq_codes", bufs=3, align_bytes=64)
            scales = work.tile([PARTS, 2 * PARTS], U8, name="hq_scales", bufs=3, align_bytes=64)
            nc.vector.quantize_mx(
                out=codes[:].bitcast(FP8X4),
                scales=scales[:],
                in_=h_grouped[pair][:].rearrange("m a n j -> m (a n j)"),
            )
            h_codes[pair], h_scales[pair] = codes, scales

        e_of, u_of = {}, {}

        def second_matmul(i, dst, codes, which):
            cols = slice(PARTS * (i % 2), PARTS * (i % 2 + 1))
            nc.tensor.matmul_mx(
                out=dst[:],
                lhsT=h_codes[i // 2][:, cols].bitcast(FP8X4),
                lhsT_scale=h_scales[i // 2][:, cols],
                rhs=codes[:].bitcast(FP4X4),
                rhs_scale=weight_scales[:, which, :],
                start=True,
                stop=True,
            )

        def scores(i):
            e_ps = psum.tile([PARTS, Q], F32, name="e_ps", bufs=3)
            e_of[i] = e_ps
            second_matmul(i, e_ps, w_codes, W)

        def mode(i):
            u_ps = psum.tile([PARTS, Q], F32, name="u_ps", bufs=2)
            u_of[i] = u_ps
            second_matmul(i, u_ps, w2_codes, W2)

        neg_max, exps, sums, factors, coeff = {}, {}, {}, {}, {}
        mixed, scaled_bias, diags, z_of = {}, {}, {}, {}

        def row_max(i):
            nmax = work.tile([PARTS, 1], F32, name="nmax", bufs=4)
            neg_max[i] = nmax
            nc.vector.tensor_reduce(out=nmax[:], in_=e_of[i][:], axis=AX.X, op=ALU.max, negate=True)

        def exponentials(i):
            e_sb = work.tile([PARTS, Q], F32, name="e_sb", bufs=4)
            e_sum = work.tile([PARTS, 1], F32, name="e_sum", bufs=10)
            exps[i], sums[i] = e_sb, e_sum
            nc.scalar.activation(
                out=e_sb[:], in_=e_of[i][:], func=ACT.Exp, bias=neg_max[i][:], scale=1.0, accum_out=e_sum[:]
            )

        def row_factors(i):
            if i % 2 == 0:
                pair = work.tile([PARTS, 2, 2], F32, name="pair", bufs=6)
                factors[i] = factors[i + 1] = pair
            nc.scalar.activation(
                out=factors[i][:, i % 2, :], in_=row_const[:, i % ROW_TILES, :], func=ACT.Copy, scale=sums[i][:]
            )

        def row_coefficients(i):
            inverse = work.tile([PARTS, 2], F32, name="inverse", bufs=8)
            coeff[i], coeff[i + 1] = inverse[:, 0:1], inverse[:, 1:2]
            nc.vector.reciprocal(out=inverse[:], in_=factors[i][:, :, 1])

        def mix(i):
            v_sb = work.tile([PARTS, Q], F32, name="v_sb", bufs=8)
            mixed[i] = v_sb
            for q in column_parts(i):
                nc.vector.scalar_tensor_tensor(
                    out=v_sb[:, q],
                    in0=exps[i][:, q],
                    scalar=factors[i][:, i % 2, 0:1],
                    in1=u_of[i][:, q],
                    op0=ALU.add,
                    op1=ALU.mult,
                )

        def bias_on_vector(i):
            z_v = work.tile([PARTS, Q], F32, name="z_v", bufs=2)
            z_of[i] = z_v
            for q in column_parts(i):
                nc.vector.scalar_tensor_tensor(
                    out=z_v[:, q],
                    in0=mixed[i][:, q],
                    scalar=coeff[i],
                    in1=bias_t[:, i % ROW_TILES, q],
                    op0=ALU.mult,
                    op1=ALU.add,
                )

        def scale_bias(i):
            bias_ys = work.tile([PARTS, Q], F32, name="bias_ys", bufs=4)
            scaled_bias[i] = bias_ys
            nc.gpsimd.tensor_scalar(
                out=bias_ys[:],
                in0=bias_t[:, i % ROW_TILES, :],
                scalar1=factors[i][:, i % 2, 1:2],
                scalar2=0.0,
                op0=ALU.mult,
                op1=ALU.add,
            )

        def bias_on_gpsimd(i):
            z_g = work.tile([PARTS, Q], F32, name="z_g", bufs=3)
            z_of[i] = z_g
            nc.gpsimd.tensor_tensor(out=z_g[:], in0=mixed[i][:], in1=scaled_bias[i][:], op=ALU.add)

        def make_diagonal(i):
            diag = work.tile([PARTS, PARTS], F32, name="diag", bufs=3)
            diags[i] = diag
            nc.gpsimd.tensor_scalar(
                out=diag[:], in0=ident_f[:], scalar1=coeff[i], scalar2=0.0, op0=ALU.mult, op1=ALU.add
            )

        def bias_on_tensor(i):
            z_ps = psum.tile([PARTS, Q], F32, name="z_ps", bufs=1)
            z_of[i] = z_ps
            nc.tensor.matmul(z_ps[:], lhsT=ident_b[:], rhs=bias_t[:, i % ROW_TILES, :], start=True, stop=False)
            nc.tensor.matmul(z_ps[:], lhsT=diags[i][:], rhs=mixed[i][:], start=False, stop=True)

        def finish(i):
            b, r = divmod(i, ROW_TILES)
            result = work.tile([PARTS, Q], F32, name="result", bufs=4)
            scale = coeff[i] if BIAS_ENGINES[i] == "g" else 1.0
            for q in column_parts(i):
                nc.scalar.activation(out=result[:, q], in_=z_of[i][:, q], func=ACT.Tanh, scale=scale)
                nc.sync.dma_start(out=out[b, PARTS * r : PARTS * (r + 1), q], in_=result[:, q])

        def is_tile(i):
            return 0 <= i < TILES

        def has_bias_on(i, engine):
            return is_tile(i) and BIAS_ENGINES[i] == engine

        for s in range(PACK):
            widen(0, s)
        for c in range(4):
            interleave(0, c)
        quantise_x(0)

        for n in range(-4, finish_step(TILES - 1) + 1):
            quantise_batch, quantise_phase = divmod(n + 4, 4)
            interleave_batch, interleave_part = divmod(n + 8, 4)
            widen_batch, widen_slot = divmod(n + 12, 4)

            if 1 <= quantise_batch < B and quantise_phase == 0:
                quantise_x(quantise_batch)
            if is_tile(n):
                row_max(n)
            for i in (n - 4, n - 3):
                if has_bias_on(i, "g") and gpsimd_bias_step(i) == n:
                    bias_on_gpsimd(i)
            if has_bias_on(n - 5, "p"):
                make_diagonal(n - 5)
            if n == -2:
                row_constants_first()
            if n == 0:
                row_constants_second()
            if has_bias_on(n - 3, "v"):
                bias_on_vector(n - 3)
            if is_tile(n - 2):
                mix(n - 2)
            if 2 <= interleave_batch < B:
                interleave(interleave_batch, interleave_part)
            if n == -4:
                for s in range(PACK):
                    widen(1, s)
                for c in range(4):
                    interleave(1, c)
            if is_tile(n + 4):
                first_matmul(n + 4)
            if is_tile(n):
                exponentials(n)
            if has_bias_on(n - 5, "p"):
                bias_on_tensor(n - 5)
            if 2 <= widen_batch < B:
                widen(widen_batch, widen_slot)
            if is_tile(n - 1):
                mode(n - 1)
            if has_bias_on(n - 2, "g"):
                scale_bias(n - 2)
            if n % 2 == 0 and is_tile(n + 2):
                quantise_h((n + 2) // 2)
            if is_tile(n):
                row_factors(n)
            if is_tile(n + 2):
                scores(n + 2)
            if is_tile(n + 4):
                apply_gain(n + 4)
            for i in range(n - 5, n - 2):
                if is_tile(i) and finish_step(i) == n:
                    finish(i)
            if n % 2 == 0 and is_tile(n - 2):
                row_coefficients(n - 2)
